import numpy as np
import ml_dtypes


def mxq(x, axis, fmt="e4m3"):
    dtype, down = {"e4m3": (ml_dtypes.float8_e4m3fn, 7), "e5m2": (ml_dtypes.float8_e5m2, 14)}[fmt]
    v = np.moveaxis(np.asarray(x, np.float32).astype(ml_dtypes.bfloat16).astype(np.float64), axis, -1)
    blocks = v.reshape(v.shape[:-1] + (-1, 32))
    amax = np.abs(blocks).max(-1, keepdims=True)
    byte = np.maximum(np.where(amax > 0, np.frexp(amax)[1] - 1 + 127, 0) - down, 1)
    scale = np.exp2(byte - 127.0)
    codes = (blocks / scale).astype(np.float32).astype(dtype).astype(np.float64)
    return np.moveaxis((codes * scale).reshape(v.shape), -1, axis)


WIDE = False


def mx_kscale(k):
    if not WIDE:
        return np.ones(k)
    levels = np.array([10, -10, 5, -5, 0])
    if k % 512:
        return np.exp2(np.random.permutation(np.resize(levels, k // 32))).repeat(32)
    a = np.empty((k // 512, 16))
    for p in range(k // 512):
        a[p, :8] = np.random.permutation(np.resize(levels, 8))
        for g in range(8):
            far = levels[np.abs(levels - a[p, g]) >= 10]
            a[p, g + 8] = far[np.random.randint(len(far))]
    return np.exp2(a.ravel()).repeat(32)


def f64(x):
    return np.asarray(x).astype(np.float64)


def striped(idx):
    return np.tile(np.asarray(idx).reshape(-1, 16).T, (8, 1)).astype(np.uint16)


def unstriped(offs):
    return offs[:16].T.reshape(-1).astype(np.int64)


E2M1 = np.array([0.0, 0.5, 1.0, 1.5, 2.0, 3.0, 4.0, 6.0, -0.0, -0.5, -1.0, -1.5, -2.0, -3.0, -4.0, -6.0])


def pack_weight(w, fmt):
    k, n = w.shape
    w = f64(np.asarray(w, np.float32).astype(ml_dtypes.bfloat16)).reshape(k // 32, 32, n)
    amax = np.abs(w).max(1)
    if fmt == "e4m3":
        byte = np.frexp(amax)[1] - 1 + 127 - 7
    else:
        mant, ex = np.frexp(amax / 6.0)
        byte = np.where(mant > 0.5, ex, ex - 1) + 127
    byte = np.clip(np.where(amax > 0, byte, 1), 1, 254)
    scaled = (w * np.exp2(127.0 - byte)[:, None, :]).reshape(k, n).astype(np.float32)
    by_word = np.ascontiguousarray(scaled.reshape(k // 512, 128, 4, n).transpose(0, 1, 3, 2))
    if fmt == "e4m3":
        words = by_word.astype(ml_dtypes.float8_e4m3fn).view(np.uint8)
    else:
        c = by_word.astype(ml_dtypes.float4_e2m1fn).view(np.uint8) & 0xF
        words = (c[..., 0::2] | (c[..., 1::2] << 4)).reshape(k // 512, 128, 2 * n)
    return np.ascontiguousarray(words), np.ascontiguousarray(byte.astype(np.uint8).reshape(k // 512, 16, n))


def unpack_weight(words, scales, fmt):
    g, _, n = scales.shape
    words = np.ascontiguousarray(words).reshape(g, 128, n, -1)
    if fmt == "e4m3":
        vals = words.view(ml_dtypes.float8_e4m3fn).astype(np.float64)
    else:
        nib = np.empty((g, 128, n, 4), np.uint8)
        nib[..., 0::2] = words & 0xF
        nib[..., 1::2] = words >> 4
        vals = E2M1[nib]
    vals = vals * np.repeat(np.exp2(scales.astype(np.float64) - 127.0), 8, axis=1)[..., None]
    return vals.transpose(0, 1, 3, 2).reshape(g * 512, n)


def bf(x):
    return np.asarray(x, np.float32).astype(ml_dtypes.bfloat16)


def planes(Y):
    r, m = Y.shape
    b = f64(bf(Y)).reshape(r // 32, 32, m)
    amax = np.abs(b).max(1)
    byte = np.clip(np.where(amax > 0, np.frexp(amax)[1] - 1 + 127 - 7, 1), 1, 254)
    codes = (b * np.exp2(127.0 - byte)[:, None, :]).reshape(r, m).astype(np.float32).astype(ml_dtypes.float8_e4m3fn).view(np.uint8)
    words = codes.reshape(r // 512, 128, 4, m).transpose(0, 1, 3, 2)
    return np.ascontiguousarray(words), np.ascontiguousarray(byte.astype(np.uint8).reshape(r // 512, 16, m))


K, T, I, F, G = 512, 2048, 1024, 512, 64


def setup_inputs():
    n = np.random.standard_normal
    idx = np.random.permutation(T)[:I]
    idx2 = np.repeat(np.random.permutation(T)[:G], I // G)
    fk = mx_kscale(K)
    ptsp = pack_weight(n((K, T)) / fk[:, None], "e4m3")
    return {
        "pts_words": ptsp[0],
        "pts_scales": ptsp[1],
        "wc": (n((K, F)) * 0.7 / np.sqrt(K) * fk[:, None]).astype(np.float32),
        "wn": (n((K, F)) * 0.7 / np.sqrt(K) * fk[:, None]).astype(np.float32),
        "bias": (0.3 * n((F, 1))).astype(np.float32),
        "offs": striped(idx),
        "offs2": striped(idx2),
    }


def reference(pts_words, pts_scales, wc, wn, bias, offs, offs2):
    idx = unstriped(offs)
    idx2 = unstriped(offs2)
    ptsu = unpack_weight(pts_words, pts_scales, "e4m3")
    wcq = mxq(f64(wc), 0, "e4m3")
    ptsidx2g = ptsu[:, idx2]
    wnq = mxq(f64(wn), 0, "e4m3")
    ptsidxg = ptsu[:, idx]
    z = wcq.T @ ptsidx2g + wnq.T @ ptsidxg
    r = np.maximum(z + f64(bias), 0.0)
    y = r.reshape(F, G, I // G).max(axis=2)
    words, scales = planes(y)
    return y, words, scales

@@ -1,0 +1,152 @@
+from contextlib import ExitStack
+
+import concourse.mybir as mybir
+
+K, T, I, F, G = 512, 2048, 1024, 512, 64
+FLOPS = 2 * 2 * K * F * I
+
+F32 = mybir.dt.float32
+BF16 = mybir.dt.bfloat16
+I32 = mybir.dt.int32
+U32 = mybir.dt.uint32
+U16 = mybir.dt.uint16
+U8 = mybir.dt.uint8
+FP8X4 = mybir.dt.float8_e4m3fn_x4
+ACT = mybir.ActivationFunctionType
+ALU = mybir.AluOpType
+AX = mybir.AxisListType
+
+P = 128
+PACK = 4
+EDGES = I // G
+N = 512
+HALVES = I // N
+W_CHUNKS = 2
+
+
+def tile_attend_edgeconv_pl_kernel(tc, pts_words, pts_scales, wc, wn, bias, offs, offs2, out_0, out_1, out_2):
+    nc = tc.nc
+    with ExitStack() as ctx:
+        keep = ctx.enter_context(tc.tile_pool(name="keep", bufs=1))
+        psum = ctx.enter_context(tc.psum_pool(name="psum", bufs=1))
+
+        list_c = keep.tile([P, I // 16], U16, name="list_c")
+        list_n = keep.tile([P, I // 16], U16, name="list_n")
+        nc.sync.dma_start(list_c[:], offs2)
+        nc.sync.dma_start(list_n[:], offs)
+
+        scales = keep.tile([P, T], U8, name="scales", align_bytes=64)
+        nc.vector.memset(scales[:].bitcast(I32), 0)
+        scale_rows = pts_scales[0].bitcast(I32).rearrange("(q r) c -> r q c", r=4)
+        for r in range(4):
+            nc.sync.dma_start(scales[:].bitcast(I32)[r:P:32, :], scale_rows[r])
+
+        cw = F // W_CHUNKS
+
+        def load_weight(w, name):
+            rows = w.rearrange("(p j) f -> p j f", j=PACK)
+            raws = []
+            for c in range(W_CHUNKS):
+                raw = keep.tile([P, PACK, cw], F32, name=f"{name}_raw{c}")
+                nc.sync.dma_start(raw[:], rows[:, :, c * cw:(c + 1) * cw])
+                raws.append(raw)
+            return raws
+
+        raw_c = load_weight(wc, "wc")
+        words = keep.tile([P, T], U32, name="words", align_bytes=64)
+        nc.sync.dma_start(words[:].bitcast(I32), pts_words[0].rearrange("p c r -> p (c r)").bitcast(I32))
+        raw_n = load_weight(wn, "wn")
+        bias_t = keep.tile([P, PACK], F32, name="bias_t")
+        nc.sync.dma_start(bias_t[:], bias.rearrange("(p t) o -> p (t o)", t=PACK))
+
+        def round_weight(raws, name):
+            dealt = keep.tile([P, PACK, P, PACK], BF16, name=f"{name}_dealt", align_bytes=64)
+            mw = cw // PACK
+            for c in range(W_CHUNKS):
+                nc.scalar.activation(
+                    out=dealt[:, :, c * mw:(c + 1) * mw, :].rearrange("p t m j -> p m t j"),
+                    in_=raws[c][:].rearrange("p j (m t) -> p m t j", t=PACK),
+                    func=ACT.Copy,
+                )
+            return dealt
+
+        def quantise_weight(dealt, name, pieces):
+            codes = keep.tile([P, F], U32, name=f"{name}_codes", align_bytes=64)
+            sc = keep.tile([P, F], U8, name=f"{name}_scales", align_bytes=64)
+            flat = dealt[:].rearrange("p t m j -> p (t m j)")
+            wd = F // pieces
+            for s in range(pieces):
+                nc.vector.quantize_mx(
+                    out=codes[:, s * wd:(s + 1) * wd].bitcast(FP8X4),
+                    scales=sc[:, s * wd:(s + 1) * wd],
+                    in_=flat[:, s * wd * PACK:(s + 1) * wd * PACK],
+                )
+            return codes, sc
+
+        gs_c = keep.tile([P, I], U8, name="gs_c", align_bytes=64)
+        gs_n = keep.tile([P, I], U8, name="gs_n", align_bytes=64)
+        nc.vector.tensor_copy(gs_c[:], scales[:].indirect(list_c[:]))
+        nc.vector.tensor_copy(gs_n[:], scales[:].indirect(list_n[:]))
+
+        dealt_c = round_weight(raw_c, "wc")
+        wc_codes, wc_sc = quantise_weight(dealt_c, "wc", 1)
+
+        gw_c = [keep.tile([P, N], U32, name=f"gw_c{h}", align_bytes=64) for h in range(HALVES)]
+        gw_n = [keep.tile([P, N], U32, name=f"gw_n{h}", align_bytes=64) for h in range(HALVES)]
+        for h in range(HALVES):
+            cols = slice(h * N // 16, (h + 1) * N // 16)
+            nc.vector.tensor_copy(gw_c[h][:], words[:].indirect(list_c[:, cols]))
+            nc.vector.tensor_copy(gw_n[h][:], words[:].indirect(list_n[:, cols]))
+
+        banks = {}
+        for h in range(HALVES):
+            for t in range(PACK):
+                banks[h, t] = psum.tile([P, N], F32, name=f"bank{h}{t}")
+                nc.tensor.matmul_mx(
+                    out=banks[h, t][:],
+                    lhsT=wc_codes[:, t * P:(t + 1) * P].bitcast(FP8X4),
+                    lhsT_scale=wc_sc[:, t * P:(t + 1) * P],
+                    rhs=gw_c[h][:].bitcast(FP8X4),
+                    rhs_scale=gs_c[:, h * N:(h + 1) * N],
+                    start=True,
+                    stop=False,
+                )
+
+        dealt_n = round_weight(raw_n, "wn")
+        wn_codes, wn_sc = quantise_weight(dealt_n, "wn", PACK)
+
+        top = keep.tile([P, PACK, G], F32, name="top")
+        y = keep.tile([P, PACK, G], F32, name="y")
+        yb = keep.tile([P, G, PACK], BF16, name="yb", align_bytes=64)
+        gh = G // HALVES
+        for h in range(HALVES):
+            for t in range(PACK):
+                nc.tensor.matmul_mx(
+                    out=banks[h, t][:],
+                    lhsT=wn_codes[:, t * P:(t + 1) * P].bitcast(FP8X4),
+                    lhsT_scale=wn_sc[:, t * P:(t + 1) * P],
+                    rhs=gw_n[h][:].bitcast(FP8X4),
+                    rhs_scale=gs_n[:, h * N:(h + 1) * N],
+                    start=False,
+                    stop=True,
+                )
+                gc = slice(h * gh, (h + 1) * gh)
+                nc.vector.tensor_reduce(
+                    out=top[:, t, gc],
+                    in_=banks[h, t][:].rearrange("p (g e) -> p g e", e=EDGES),
+                    axis=AX.X,
+                    op=ALU.max,
+                )
+                nc.scalar.activation(out=yb[:, gc, t], in_=top[:, t, gc], func=ACT.Relu, bias=bias_t[:, t:t + 1])
+                nc.scalar.activation(out=y[:, t, gc], in_=top[:, t, gc], func=ACT.Relu, bias=bias_t[:, t:t + 1])
+
+        y_codes = keep.tile([P, G], U32, name="y_codes", align_bytes=64)
+        y_sc = keep.tile([P, G], U8, name="y_sc", align_bytes=64)
+        nc.vector.quantize_mx(out=y_codes[:].bitcast(FP8X4), scales=y_sc[:], in_=yb[:].rearrange("p g t -> p (g t)"))
+
+        nc.scalar.dma_start(out_0.rearrange("(p t) g -> p t g", t=PACK), y[:])
+        nc.sync.dma_start(out_1[0].rearrange("p g r -> p (g r)").bitcast(I32), y_codes[:].bitcast(I32))
+        out_rows = out_2[0].bitcast(I32).rearrange("(q r) c -> q r c", r=4)
+        for q in range(4):
+            queue = nc.sync if q % 2 == 0 else nc.scalar
+            queue.dma_start(out_rows[q], y_sc[:].bitcast(I32)[32 * q:32 * q + 4, :])

@@ -22,6 +22,7 @@ EDGES = I // G
 N = 512
 HALVES = I // N
 W_CHUNKS = 2
+LATE = 8
 
 
 def tile_attend_edgeconv_pl_kernel(tc, pts_words, pts_scales, wc, wn, bias, offs, offs2, out_0, out_1, out_2):
@@ -39,7 +40,8 @@ def tile_attend_edgeconv_pl_kernel(tc, pts_words, pts_scales, wc, wn, bias, offs
         nc.vector.memset(scales[:].bitcast(I32), 0)
         scale_rows = pts_scales[0].bitcast(I32).rearrange("(q r) c -> r q c", r=4)
         for r in range(4):
-            nc.sync.dma_start(scales[:].bitcast(I32)[r:P:32, :], scale_rows[r])
+            queue = nc.sync if r % 2 == 0 else nc.scalar
+            queue.dma_start(scales[:].bitcast(I32)[r:P:32, :], scale_rows[r])
 
         cw = F // W_CHUNKS
 
@@ -47,7 +49,7 @@ def tile_attend_edgeconv_pl_kernel(tc, pts_words, pts_scales, wc, wn, bias, offs
             rows = w.rearrange("(p j) f -> p j f", j=PACK)
             raws = []
             for c in range(W_CHUNKS):
-                raw = keep.tile([P, PACK, cw], F32, name=f"{name}_raw{c}")
+                raw = keep.tile([P, PACK, cw], F32, name=f"{name}_raw{c}", tag=f"{name}_raw{c}", align_bytes=64)
                 nc.sync.dma_start(raw[:], rows[:, :, c * cw:(c + 1) * cw])
                 raws.append(raw)
             return raws
@@ -92,11 +94,11 @@ def tile_attend_edgeconv_pl_kernel(tc, pts_words, pts_scales, wc, wn, bias, offs
         wc_codes, wc_sc = quantise_weight(dealt_c, "wc", 1)
 
         gw_c = [keep.tile([P, N], U32, name=f"gw_c{h}", align_bytes=64) for h in range(HALVES)]
-        gw_n = [keep.tile([P, N], U32, name=f"gw_n{h}", align_bytes=64) for h in range(HALVES)]
+        gw_n = [keep.tile([P, N], U32, name="gw_n0", align_bytes=64)]
+        cols = [slice(h * N // 16, (h + 1) * N // 16) for h in range(HALVES)]
         for h in range(HALVES):
-            cols = slice(h * N // 16, (h + 1) * N // 16)
-            nc.vector.tensor_copy(gw_c[h][:], words[:].indirect(list_c[:, cols]))
-            nc.vector.tensor_copy(gw_n[h][:], words[:].indirect(list_n[:, cols]))
+            nc.vector.tensor_copy(gw_c[h][:], words[:].indirect(list_c[:, cols[h]]))
+        nc.vector.tensor_copy(gw_n[0][:], words[:].indirect(list_n[:, cols[0]]))
 
         banks = {}
         for h in range(HALVES):
@@ -113,11 +115,14 @@ def tile_attend_edgeconv_pl_kernel(tc, pts_words, pts_scales, wc, wn, bias, offs
                 )
 
         dealt_n = round_weight(raw_n, "wn")
-        wn_codes, wn_sc = quantise_weight(dealt_n, "wn", PACK)
+        wn_codes, wn_sc = quantise_weight(dealt_n, "wn", 2)
+        gw_n.append(keep.tile([P, N], U32, name="gw_n1", tag=f"wn_raw{W_CHUNKS - 1}", align_bytes=64))
+        nc.vector.tensor_copy(gw_n[1][:], words[:].indirect(list_n[:, cols[1]]))
 
         top = keep.tile([P, PACK, G], F32, name="top")
         y = keep.tile([P, PACK, G], F32, name="y")
         yb = keep.tile([P, G, PACK], BF16, name="yb", align_bytes=64)
+        rel = keep.tile([P, 2, LATE * EDGES], F32, name="rel")
         gh = G // HALVES
         for h in range(HALVES):
             for t in range(PACK):
@@ -130,21 +135,41 @@ def tile_attend_edgeconv_pl_kernel(tc, pts_words, pts_scales, wc, wn, bias, offs
                     start=False,
                     stop=True,
                 )
-                gc = slice(h * gh, (h + 1) * gh)
+        for u in range(2):
+            t = PACK - 2 + u
+            nc.scalar.activation(out=rel[:, u, :], in_=banks[HALVES - 1, t][:, N - LATE * EDGES:], func=ACT.Relu, bias=bias_t[:, t:t + 1])
+        for h in range(HALVES):
+            for t in range(PACK):
+                count = gh - LATE if h == HALVES - 1 and t >= PACK - 2 else gh
+                gc = slice(h * gh, h * gh + count)
                 nc.vector.tensor_reduce(
                     out=top[:, t, gc],
-                    in_=banks[h, t][:].rearrange("p (g e) -> p g e", e=EDGES),
+                    in_=banks[h, t][:, 0:count * EDGES].rearrange("p (g e) -> p g e", e=EDGES),
                     axis=AX.X,
                     op=ALU.max,
                 )
                 nc.scalar.activation(out=yb[:, gc, t], in_=top[:, t, gc], func=ACT.Relu, bias=bias_t[:, t:t + 1])
                 nc.scalar.activation(out=y[:, t, gc], in_=top[:, t, gc], func=ACT.Relu, bias=bias_t[:, t:t + 1])
+        nc.vector.tensor_reduce(
+            out=yb[:, G - LATE:, PACK - 2:],
+            in_=rel[:].rearrange("p u (g e) -> p g u e", e=EDGES),
+            axis=AX.X,
+            op=ALU.max,
+        )
+        nc.vector.tensor_reduce(
+            out=y[:, PACK - 2:, G - LATE:],
+            in_=rel[:].rearrange("p u (g e) -> p u g e", e=EDGES),
+            axis=AX.X,
+            op=ALU.max,
+        )
 
         y_codes = keep.tile([P, G], U32, name="y_codes", align_bytes=64)
         y_sc = keep.tile([P, G], U8, name="y_sc", align_bytes=64)
         nc.vector.quantize_mx(out=y_codes[:].bitcast(FP8X4), scales=y_sc[:], in_=yb[:].rearrange("p g t -> p (g t)"))
 
-        nc.scalar.dma_start(out_0.rearrange("(p t) g -> p t g", t=PACK), y[:])
+        out_dealt = out_0.rearrange("(p t) g -> p t g", t=PACK)
+        nc.sync.dma_start(out_dealt[:, 0:PACK - 2, :], y[:, 0:PACK - 2, :])
+        nc.scalar.dma_start(out_dealt[:, PACK - 2:, :], y[:, PACK - 2:, :])
         nc.sync.dma_start(out_1[0].rearrange("p g r -> p (g r)").bitcast(I32), y_codes[:].bitcast(I32))
         out_rows = out_2[0].bitcast(I32).rearrange("(q r) c -> q r c", r=4)
         for q in range(4):

@@ -27,6 +27,7 @@ LATE = 8
 
 def tile_attend_edgeconv_pl_kernel(tc, pts_words, pts_scales, wc, wn, bias, offs, offs2, out_0, out_1, out_2):
     nc = tc.nc
+    wc, wn, offs, offs2 = wn, wc, offs2, offs
     with ExitStack() as ctx:
         keep = ctx.enter_context(tc.tile_pool(name="keep", bufs=1))
         psum = ctx.enter_context(tc.psum_pool(name="psum", bufs=1))

@@ -21,13 +21,13 @@ PACK = 4
 EDGES = I // G
 N = 512
 HALVES = I // N
-W_CHUNKS = 2
+WC_CHUNKS = (256, 256)
+WN_CHUNKS = (128, 192, 192)
 LATE = 8
 
 
 def tile_attend_edgeconv_pl_kernel(tc, pts_words, pts_scales, wc, wn, bias, offs, offs2, out_0, out_1, out_2):
     nc = tc.nc
-    wc, wn, offs, offs2 = wn, wc, offs2, offs
     with ExitStack() as ctx:
         keep = ctx.enter_context(tc.tile_pool(name="keep", bufs=1))
         psum = ctx.enter_context(tc.psum_pool(name="psum", bufs=1))
@@ -44,30 +44,27 @@ def tile_attend_edgeconv_pl_kernel(tc, pts_words, pts_scales, wc, wn, bias, offs
             queue = nc.sync if r % 2 == 0 else nc.scalar
             queue.dma_start(scales[:].bitcast(I32)[r:P:32, :], scale_rows[r])
 
-        cw = F // W_CHUNKS
-
-        def load_weight(w, name):
+        def load_chunk(w, name, widths, c):
             rows = w.rearrange("(p j) f -> p j f", j=PACK)
-            raws = []
-            for c in range(W_CHUNKS):
-                raw = keep.tile([P, PACK, cw], F32, name=f"{name}_raw{c}", tag=f"{name}_raw{c}", align_bytes=64)
-                nc.sync.dma_start(raw[:], rows[:, :, c * cw:(c + 1) * cw])
-                raws.append(raw)
-            return raws
+            f0 = sum(widths[:c])
+            raw = keep.tile([P, PACK, widths[c]], F32, name=f"{name}_raw{c}", tag=f"{name}_raw{c}", align_bytes=64)
+            nc.sync.dma_start(raw[:], rows[:, :, f0:f0 + widths[c]])
+            return raw
 
-        raw_c = load_weight(wc, "wc")
+        raw_c = [load_chunk(wc, "wc", WC_CHUNKS, c) for c in range(len(WC_CHUNKS))]
+        raw_n = [load_chunk(wn, "wn", WN_CHUNKS, 0)]
         words = keep.tile([P, T], U32, name="words", align_bytes=64)
         nc.sync.dma_start(words[:].bitcast(I32), pts_words[0].rearrange("p c r -> p (c r)").bitcast(I32))
-        raw_n = load_weight(wn, "wn")
+        raw_n.extend(load_chunk(wn, "wn", WN_CHUNKS, c) for c in range(1, len(WN_CHUNKS)))
         bias_t = keep.tile([P, PACK], F32, name="bias_t")
         nc.sync.dma_start(bias_t[:], bias.rearrange("(p t) o -> p (t o)", t=PACK))
 
-        def round_weight(raws, name):
+        def round_weight(raws, name, widths):
             dealt = keep.tile([P, PACK, P, PACK], BF16, name=f"{name}_dealt", align_bytes=64)
-            mw = cw // PACK
-            for c in range(W_CHUNKS):
+            for c in range(len(widths)):
+                m0 = sum(widths[:c]) // PACK
                 nc.scalar.activation(
-                    out=dealt[:, :, c * mw:(c + 1) * mw, :].rearrange("p t m j -> p m t j"),
+                    out=dealt[:, :, m0:m0 + widths[c] // PACK, :].rearrange("p t m j -> p m t j"),
                     in_=raws[c][:].rearrange("p j (m t) -> p m t j", t=PACK),
                     func=ACT.Copy,
                 )
@@ -88,54 +85,54 @@ def tile_attend_edgeconv_pl_kernel(tc, pts_words, pts_scales, wc, wn, bias, offs
 
         gs_c = keep.tile([P, I], U8, name="gs_c", align_bytes=64)
         gs_n = keep.tile([P, I], U8, name="gs_n", align_bytes=64)
-        nc.vector.tensor_copy(gs_c[:], scales[:].indirect(list_c[:]))
         nc.vector.tensor_copy(gs_n[:], scales[:].indirect(list_n[:]))
+        nc.vector.tensor_copy(gs_c[:], scales[:].indirect(list_c[:]))
 
-        dealt_c = round_weight(raw_c, "wc")
+        dealt_c = round_weight(raw_c, "wc", WC_CHUNKS)
         wc_codes, wc_sc = quantise_weight(dealt_c, "wc", 1)
 
-        gw_c = [keep.tile([P, N], U32, name=f"gw_c{h}", align_bytes=64) for h in range(HALVES)]
-        gw_n = [keep.tile([P, N], U32, name="gw_n0", align_bytes=64)]
+        gw_c = [keep.tile([P, N], U32, name="gw_c0", align_bytes=64)]
+        gw_n = [keep.tile([P, N], U32, name=f"gw_n{h}", align_bytes=64) for h in range(HALVES)]
         cols = [slice(h * N // 16, (h + 1) * N // 16) for h in range(HALVES)]
+        nc.vector.tensor_copy(gw_c[0][:], words[:].indirect(list_c[:, cols[0]]))
         for h in range(HALVES):
-            nc.vector.tensor_copy(gw_c[h][:], words[:].indirect(list_c[:, cols[h]]))
-        nc.vector.tensor_copy(gw_n[0][:], words[:].indirect(list_n[:, cols[0]]))
+            nc.vector.tensor_copy(gw_n[h][:], words[:].indirect(list_n[:, cols[h]]))
 
         banks = {}
         for h in range(HALVES):
             for t in range(PACK):
                 banks[h, t] = psum.tile([P, N], F32, name=f"bank{h}{t}")
-                nc.tensor.matmul_mx(
-                    out=banks[h, t][:],
-                    lhsT=wc_codes[:, t * P:(t + 1) * P].bitcast(FP8X4),
-                    lhsT_scale=wc_sc[:, t * P:(t + 1) * P],
-                    rhs=gw_c[h][:].bitcast(FP8X4),
-                    rhs_scale=gs_c[:, h * N:(h + 1) * N],
-                    start=True,
-                    stop=False,
-                )
 
-        dealt_n = round_weight(raw_n, "wn")
-        wn_codes, wn_sc = quantise_weight(dealt_n, "wn", 2)
-        gw_n.append(keep.tile([P, N], U32, name="gw_n1", tag=f"wn_raw{W_CHUNKS - 1}", align_bytes=64))
-        nc.vector.tensor_copy(gw_n[1][:], words[:].indirect(list_n[:, cols[1]]))
+        def product(h, t, codes, sc, gw, gs, first):
+            nc.tensor.matmul_mx(
+                out=banks[h, t][:],
+                lhsT=codes[:, t * P:(t + 1) * P].bitcast(FP8X4),
+                lhsT_scale=sc[:, t * P:(t + 1) * P],
+                rhs=gw[h][:].bitcast(FP8X4),
+                rhs_scale=gs[:, h * N:(h + 1) * N],
+                start=first,
+                stop=not first,
+            )
+
+        for t in range(PACK):
+            product(0, t, wc_codes, wc_sc, gw_c, gs_c, True)
+
+        dealt_n = round_weight(raw_n, "wn", WN_CHUNKS)
+        wn_codes, wn_sc = quantise_weight(dealt_n, "wn", PACK)
+        gw_c.append(keep.tile([P, N], U32, name="gw_c1", tag=f"wn_raw{len(WN_CHUNKS) - 1}", align_bytes=64))
+        nc.vector.tensor_copy(gw_c[1][:], words[:].indirect(list_c[:, cols[1]]))
+
+        for t in range(PACK):
+            product(0, t, wn_codes, wn_sc, gw_n, gs_n, False)
+        for t in range(PACK):
+            product(1, t, wn_codes, wn_sc, gw_n, gs_n, True)
+            product(1, t, wc_codes, wc_sc, gw_c, gs_c, False)
 
         top = keep.tile([P, PACK, G], F32, name="top")
         y = keep.tile([P, PACK, G], F32, name="y")
         yb = keep.tile([P, G, PACK], BF16, name="yb", align_bytes=64)
         rel = keep.tile([P, 2, LATE * EDGES], F32, name="rel")
         gh = G // HALVES
-        for h in range(HALVES):
-            for t in range(PACK):
-                nc.tensor.matmul_mx(
-                    out=banks[h, t][:],
-                    lhsT=wn_codes[:, t * P:(t + 1) * P].bitcast(FP8X4),
-                    lhsT_scale=wn_sc[:, t * P:(t + 1) * P],
-                    rhs=gw_n[h][:].bitcast(FP8X4),
-                    rhs_scale=gs_n[:, h * N:(h + 1) * N],
-                    start=False,
-                    stop=True,
-                )
         for u in range(2):
             t = PACK - 2 + u
             nc.scalar.activation(out=rel[:, u, :], in_=banks[HALVES - 1, t][:, N - LATE * EDGES:], func=ACT.Relu, bias=bias_t[:, t:t + 1])

@@ -63,11 +63,12 @@ def tile_attend_edgeconv_pl_kernel(tc, pts_words, pts_scales, wc, wn, bias, offs
             dealt = keep.tile([P, PACK, P, PACK], BF16, name=f"{name}_dealt", align_bytes=64)
             for c in range(len(widths)):
                 m0 = sum(widths[:c]) // PACK
-                nc.scalar.activation(
-                    out=dealt[:, :, m0:m0 + widths[c] // PACK, :].rearrange("p t m j -> p m t j"),
-                    in_=raws[c][:].rearrange("p j (m t) -> p m t j", t=PACK),
-                    func=ACT.Copy,
-                )
+                for t0 in range(0, PACK, 2):
+                    nc.scalar.activation(
+                        out=dealt[:, t0:t0 + 2, m0:m0 + widths[c] // PACK, :].rearrange("p t m j -> p m j t"),
+                        in_=raws[c][:].rearrange("p j (m t) -> p m j t", t=PACK)[:, :, :, t0:t0 + 2],
+                        func=ACT.Copy,
+                    )
             return dealt
 
         def quantise_weight(dealt, name, pieces):

@@ -52,10 +52,9 @@ def tile_attend_edgeconv_pl_kernel(tc, pts_words, pts_scales, wc, wn, bias, offs
             return raw
 
         raw_c = [load_chunk(wc, "wc", WC_CHUNKS, c) for c in range(len(WC_CHUNKS))]
-        raw_n = [load_chunk(wn, "wn", WN_CHUNKS, 0)]
         words = keep.tile([P, T], U32, name="words", align_bytes=64)
         nc.sync.dma_start(words[:].bitcast(I32), pts_words[0].rearrange("p c r -> p (c r)").bitcast(I32))
-        raw_n.extend(load_chunk(wn, "wn", WN_CHUNKS, c) for c in range(1, len(WN_CHUNKS)))
+        raw_n = [load_chunk(wn, "wn", WN_CHUNKS, c) for c in range(len(WN_CHUNKS))]
         bias_t = keep.tile([P, PACK], F32, name="bias_t")
         nc.sync.dma_start(bias_t[:], bias.rearrange("(p t) o -> p (t o)", t=PACK))
 

@@ -23,7 +23,7 @@ N = 512
 HALVES = I // N
 WC_CHUNKS = (256, 256)
 WN_CHUNKS = (128, 192, 192)
-LATE = 8
+SHARED = 16
 
 
 def tile_attend_edgeconv_pl_kernel(tc, pts_words, pts_scales, wc, wn, bias, offs, offs2, out_0, out_1, out_2):
@@ -92,11 +92,11 @@ def tile_attend_edgeconv_pl_kernel(tc, pts_words, pts_scales, wc, wn, bias, offs
         wc_codes, wc_sc = quantise_weight(dealt_c, "wc", 1)
 
         gw_c = [keep.tile([P, N], U32, name="gw_c0", align_bytes=64)]
-        gw_n = [keep.tile([P, N], U32, name=f"gw_n{h}", align_bytes=64) for h in range(HALVES)]
+        gw_all = keep.tile([P, I], U32, name="gw_n", align_bytes=64)
+        gw_n = [gw_all[:, h * N:(h + 1) * N] for h in range(HALVES)]
         cols = [slice(h * N // 16, (h + 1) * N // 16) for h in range(HALVES)]
         nc.vector.tensor_copy(gw_c[0][:], words[:].indirect(list_c[:, cols[0]]))
-        for h in range(HALVES):
-            nc.vector.tensor_copy(gw_n[h][:], words[:].indirect(list_n[:, cols[h]]))
+        nc.vector.tensor_copy(gw_all[:], words[:].indirect(list_n[:]))
 
         banks = {}
         for h in range(HALVES):
@@ -131,43 +131,48 @@ def tile_attend_edgeconv_pl_kernel(tc, pts_words, pts_scales, wc, wn, bias, offs
         top = keep.tile([P, PACK, G], F32, name="top")
         y = keep.tile([P, PACK, G], F32, name="y")
         yb = keep.tile([P, G, PACK], BF16, name="yb", align_bytes=64)
-        rel = keep.tile([P, 2, LATE * EDGES], F32, name="rel")
+        half = EDGES // 2
+        rel = keep.tile([P, 2, SHARED, EDGES], F32, name="rel")
+        diff = keep.tile([P, 2, SHARED, half], F32, name="diff")
+        excess = keep.tile([P, 2, SHARED, half], F32, name="excess")
+        pair_max = keep.tile([P, 2, SHARED, half], F32, name="pair_max")
         gh = G // HALVES
         for u in range(2):
-            t = PACK - 2 + u
-            nc.scalar.activation(out=rel[:, u, :], in_=banks[HALVES - 1, t][:, N - LATE * EDGES:], func=ACT.Relu, bias=bias_t[:, t:t + 1])
-        for h in range(HALVES):
-            for t in range(PACK):
-                count = gh - LATE if h == HALVES - 1 and t >= PACK - 2 else gh
-                gc = slice(h * gh, h * gh + count)
-                nc.vector.tensor_reduce(
-                    out=top[:, t, gc],
-                    in_=banks[h, t][:, 0:count * EDGES].rearrange("p (g e) -> p g e", e=EDGES),
-                    axis=AX.X,
-                    op=ALU.max,
-                )
-                nc.scalar.activation(out=yb[:, gc, t], in_=top[:, t, gc], func=ACT.Relu, bias=bias_t[:, t:t + 1])
-                nc.scalar.activation(out=y[:, t, gc], in_=top[:, t, gc], func=ACT.Relu, bias=bias_t[:, t:t + 1])
+            nc.scalar.activation(
+                out=rel[:, u].rearrange("p g e -> p (g e)"), in_=banks[0, 2 + u][:, 0:SHARED * EDGES], func=ACT.Relu, bias=bias_t[:, 2 + u:3 + u]
+            )
+        for t in range(2):
+            nc.gpsimd.tensor_tensor(diff[:, t], rel[:, t, :, 0:half], rel[:, t, :, half:], ALU.subtract)
+        for t in range(2):
+            nc.scalar.activation(out=excess[:, t], in_=diff[:, t], func=ACT.Relu)
+        for t in range(2):
+            nc.gpsimd.tensor_tensor(pair_max[:, t], excess[:, t], rel[:, t, :, half:], ALU.add)
+        for h, t in [(h, t) for h in range(HALVES) for t in range(PACK)]:
+            skip = SHARED if h == 0 and t >= 2 else 0
+            gc = slice(h * gh + skip, (h + 1) * gh)
+            nc.vector.tensor_reduce(
+                out=top[:, t, gc],
+                in_=banks[h, t][:, skip * EDGES:].rearrange("p (g e) -> p g e", e=EDGES),
+                axis=AX.X,
+                op=ALU.max,
+            )
+            nc.scalar.activation(out=yb[:, gc, t], in_=top[:, t, gc], func=ACT.Relu, bias=bias_t[:, t:t + 1])
+            nc.scalar.activation(out=y[:, t, gc], in_=top[:, t, gc], func=ACT.Relu, bias=bias_t[:, t:t + 1])
         nc.vector.tensor_reduce(
-            out=yb[:, G - LATE:, PACK - 2:],
-            in_=rel[:].rearrange("p u (g e) -> p g u e", e=EDGES),
+            out=yb[:, 0:SHARED, 2:],
+            in_=pair_max[:].rearrange("p u g e -> p g u e"),
             axis=AX.X,
             op=ALU.max,
         )
-        nc.vector.tensor_reduce(
-            out=y[:, PACK - 2:, G - LATE:],
-            in_=rel[:].rearrange("p u (g e) -> p u g e", e=EDGES),
-            axis=AX.X,
-            op=ALU.max,
-        )
+        nc.vector.tensor_reduce(out=y[:, 2:, 0:SHARED], in_=pair_max[:], axis=AX.X, op=ALU.max)
 
         y_codes = keep.tile([P, G], U32, name="y_codes", align_bytes=64)
         y_sc = keep.tile([P, G], U8, name="y_sc", align_bytes=64)
         nc.vector.quantize_mx(out=y_codes[:].bitcast(FP8X4), scales=y_sc[:], in_=yb[:].rearrange("p g t -> p (g t)"))
 
         out_dealt = out_0.rearrange("(p t) g -> p t g", t=PACK)
-        nc.sync.dma_start(out_dealt[:, 0:PACK - 2, :], y[:, 0:PACK - 2, :])
-        nc.scalar.dma_start(out_dealt[:, PACK - 2:, :], y[:, PACK - 2:, :])
+        nc.sync.dma_start(out_dealt[:, 0:2, :], y[:, 0:2, :])
+        nc.scalar.dma_start(out_dealt[:, 2:, :], y[:, 2:, :])
         nc.sync.dma_start(out_1[0].rearrange("p g r -> p (g r)").bitcast(I32), y_codes[:].bitcast(I32))
         out_rows = out_2[0].bitcast(I32).rearrange("(q r) c -> q r c", r=4)
         for q in range(4):

@@ -21,9 +21,12 @@ PACK = 4
 EDGES = I // G
 N = 512
 HALVES = I // N
+LIST_ROWS = 16
+QUADRANT = 32
 WC_CHUNKS = (256, 256)
 WN_CHUNKS = (128, 192, 192)
 SHARED = 16
+SHARED_BANKS = (0, 2, 3)
 
 
 def tile_attend_edgeconv_pl_kernel(tc, pts_words, pts_scales, wc, wn, bias, offs, offs2, out_0, out_1, out_2):
@@ -32,39 +35,42 @@ def tile_attend_edgeconv_pl_kernel(tc, pts_words, pts_scales, wc, wn, bias, offs
         keep = ctx.enter_context(tc.tile_pool(name="keep", bufs=1))
         psum = ctx.enter_context(tc.psum_pool(name="psum", bufs=1))
 
-        list_c = keep.tile([P, I // 16], U16, name="list_c")
-        list_n = keep.tile([P, I // 16], U16, name="list_n")
+        list_c = keep.tile([P, I // LIST_ROWS], U16, name="list_c")
+        list_n = keep.tile([P, I // LIST_ROWS], U16, name="list_n")
         nc.sync.dma_start(list_c[:], offs2)
         nc.sync.dma_start(list_n[:], offs)
 
         scales = keep.tile([P, T], U8, name="scales", align_bytes=64)
         nc.vector.memset(scales[:].bitcast(I32), 0)
-        scale_rows = pts_scales[0].bitcast(I32).rearrange("(q r) c -> r q c", r=4)
-        for r in range(4):
+        scale_rows = pts_scales[0].bitcast(I32).rearrange("(q r) c -> r q c", r=PACK)
+        for r in range(PACK):
             queue = nc.sync if r % 2 == 0 else nc.scalar
-            queue.dma_start(scales[:].bitcast(I32)[r:P:32, :], scale_rows[r])
+            queue.dma_start(scales[:].bitcast(I32)[r:P:QUADRANT, :], scale_rows[r])
 
-        def load_chunk(w, name, widths, c):
+        def load_weight(w, name, widths):
             rows = w.rearrange("(p j) f -> p j f", j=PACK)
-            f0 = sum(widths[:c])
-            raw = keep.tile([P, PACK, widths[c]], F32, name=f"{name}_raw{c}", tag=f"{name}_raw{c}", align_bytes=64)
-            nc.sync.dma_start(raw[:], rows[:, :, f0:f0 + widths[c]])
-            return raw
+            raws = []
+            for c, width in enumerate(widths):
+                f0 = sum(widths[:c])
+                raw = keep.tile([P, PACK, width], F32, name=f"{name}_raw{c}", tag=f"{name}_raw{c}", align_bytes=64)
+                nc.sync.dma_start(raw[:], rows[:, :, f0:f0 + width])
+                raws.append(raw)
+            return raws
 
-        raw_c = [load_chunk(wc, "wc", WC_CHUNKS, c) for c in range(len(WC_CHUNKS))]
+        raw_c = load_weight(wc, "wc", WC_CHUNKS)
         words = keep.tile([P, T], U32, name="words", align_bytes=64)
         nc.sync.dma_start(words[:].bitcast(I32), pts_words[0].rearrange("p c r -> p (c r)").bitcast(I32))
-        raw_n = [load_chunk(wn, "wn", WN_CHUNKS, c) for c in range(len(WN_CHUNKS))]
+        raw_n = load_weight(wn, "wn", WN_CHUNKS)
         bias_t = keep.tile([P, PACK], F32, name="bias_t")
         nc.sync.dma_start(bias_t[:], bias.rearrange("(p t) o -> p (t o)", t=PACK))
 
         def round_weight(raws, name, widths):
             dealt = keep.tile([P, PACK, P, PACK], BF16, name=f"{name}_dealt", align_bytes=64)
-            for c in range(len(widths)):
+            for c, width in enumerate(widths):
                 m0 = sum(widths[:c]) // PACK
                 for t0 in range(0, PACK, 2):
                     nc.scalar.activation(
-                        out=dealt[:, t0:t0 + 2, m0:m0 + widths[c] // PACK, :].rearrange("p t m j -> p m j t"),
+                        out=dealt[:, t0:t0 + 2, m0:m0 + width // PACK, :].rearrange("p t m j -> p m j t"),
                         in_=raws[c][:].rearrange("p j (m t) -> p m j t", t=PACK)[:, :, :, t0:t0 + 2],
                         func=ACT.Copy,
                     )
@@ -74,12 +80,12 @@ def tile_attend_edgeconv_pl_kernel(tc, pts_words, pts_scales, wc, wn, bias, offs
             codes = keep.tile([P, F], U32, name=f"{name}_codes", align_bytes=64)
             sc = keep.tile([P, F], U8, name=f"{name}_scales", align_bytes=64)
             flat = dealt[:].rearrange("p t m j -> p (t m j)")
-            wd = F // pieces
+            width = F // pieces
             for s in range(pieces):
                 nc.vector.quantize_mx(
-                    out=codes[:, s * wd:(s + 1) * wd].bitcast(FP8X4),
-                    scales=sc[:, s * wd:(s + 1) * wd],
-                    in_=flat[:, s * wd * PACK:(s + 1) * wd * PACK],
+                    out=codes[:, s * width:(s + 1) * width].bitcast(FP8X4),
+                    scales=sc[:, s * width:(s + 1) * width],
+                    in_=flat[:, s * width * PACK:(s + 1) * width * PACK],
                 )
             return codes, sc
 
@@ -91,27 +97,27 @@ def tile_attend_edgeconv_pl_kernel(tc, pts_words, pts_scales, wc, wn, bias, offs
         dealt_c = round_weight(raw_c, "wc", WC_CHUNKS)
         wc_codes, wc_sc = quantise_weight(dealt_c, "wc", 1)
 
-        gw_c = [keep.tile([P, N], U32, name="gw_c0", align_bytes=64)]
-        gw_all = keep.tile([P, I], U32, name="gw_n", align_bytes=64)
-        gw_n = [gw_all[:, h * N:(h + 1) * N] for h in range(HALVES)]
-        cols = [slice(h * N // 16, (h + 1) * N // 16) for h in range(HALVES)]
-        nc.vector.tensor_copy(gw_c[0][:], words[:].indirect(list_c[:, cols[0]]))
-        nc.vector.tensor_copy(gw_all[:], words[:].indirect(list_n[:]))
+        gw_early = keep.tile([P, N + I], U32, name="gw_early", tag=f"wc_raw{len(WC_CHUNKS) - 1}", align_bytes=64)
+        gw_c = [gw_early[:, 0:N]]
+        gw_n = [gw_early[:, (h + 1) * N:(h + 2) * N] for h in range(HALVES)]
+        half_cols = N // LIST_ROWS
+        nc.vector.tensor_copy(gw_c[0][:], words[:].indirect(list_c[:, 0:half_cols]))
+        nc.vector.tensor_copy(gw_early[:, N:], words[:].indirect(list_n[:]))
 
         banks = {}
         for h in range(HALVES):
             for t in range(PACK):
                 banks[h, t] = psum.tile([P, N], F32, name=f"bank{h}{t}")
 
-        def product(h, t, codes, sc, gw, gs, first):
+        def product(h, t, codes, sc, gw, gs, opens):
             nc.tensor.matmul_mx(
                 out=banks[h, t][:],
                 lhsT=codes[:, t * P:(t + 1) * P].bitcast(FP8X4),
                 lhsT_scale=sc[:, t * P:(t + 1) * P],
                 rhs=gw[h][:].bitcast(FP8X4),
                 rhs_scale=gs[:, h * N:(h + 1) * N],
-                start=first,
-                stop=not first,
+                start=opens,
+                stop=not opens,
             )
 
         for t in range(PACK):
@@ -120,7 +126,7 @@ def tile_attend_edgeconv_pl_kernel(tc, pts_words, pts_scales, wc, wn, bias, offs
         dealt_n = round_weight(raw_n, "wn", WN_CHUNKS)
         wn_codes, wn_sc = quantise_weight(dealt_n, "wn", PACK)
         gw_c.append(keep.tile([P, N], U32, name="gw_c1", tag=f"wn_raw{len(WN_CHUNKS) - 1}", align_bytes=64))
-        nc.vector.tensor_copy(gw_c[1][:], words[:].indirect(list_c[:, cols[1]]))
+        nc.vector.tensor_copy(gw_c[1][:], words[:].indirect(list_c[:, half_cols:]))
 
         for t in range(PACK):
             product(0, t, wn_codes, wn_sc, gw_n, gs_n, False)
@@ -131,40 +137,56 @@ def tile_attend_edgeconv_pl_kernel(tc, pts_words, pts_scales, wc, wn, bias, offs
         top = keep.tile([P, PACK, G], F32, name="top")
         y = keep.tile([P, PACK, G], F32, name="y")
         yb = keep.tile([P, G, PACK], BF16, name="yb", align_bytes=64)
-        half = EDGES // 2
-        rel = keep.tile([P, 2, SHARED, EDGES], F32, name="rel")
-        diff = keep.tile([P, 2, SHARED, half], F32, name="diff")
-        excess = keep.tile([P, 2, SHARED, half], F32, name="excess")
-        pair_max = keep.tile([P, 2, SHARED, half], F32, name="pair_max")
         gh = G // HALVES
-        for u in range(2):
+        pair = EDGES // 2
+
+        shares = len(SHARED_BANKS)
+        rel = keep.tile([P, shares, SHARED, EDGES], F32, name="rel")
+        diff = keep.tile([P, shares, SHARED, pair], F32, name="diff")
+        excess = keep.tile([P, shares, SHARED, pair], F32, name="excess")
+        pair_max = keep.tile([P, shares, SHARED, pair], F32, name="pair_max")
+        for s, t in enumerate(SHARED_BANKS):
             nc.scalar.activation(
-                out=rel[:, u].rearrange("p g e -> p (g e)"), in_=banks[0, 2 + u][:, 0:SHARED * EDGES], func=ACT.Relu, bias=bias_t[:, 2 + u:3 + u]
+                out=rel[:, s].rearrange("p g e -> p (g e)"),
+                in_=banks[0, t][:, 0:SHARED * EDGES],
+                func=ACT.Relu,
+                bias=bias_t[:, t:t + 1],
             )
-        for t in range(2):
-            nc.gpsimd.tensor_tensor(diff[:, t], rel[:, t, :, 0:half], rel[:, t, :, half:], ALU.subtract)
-        for t in range(2):
-            nc.scalar.activation(out=excess[:, t], in_=diff[:, t], func=ACT.Relu)
-        for t in range(2):
-            nc.gpsimd.tensor_tensor(pair_max[:, t], excess[:, t], rel[:, t, :, half:], ALU.add)
-        for h, t in [(h, t) for h in range(HALVES) for t in range(PACK)]:
-            skip = SHARED if h == 0 and t >= 2 else 0
-            gc = slice(h * gh + skip, (h + 1) * gh)
+        for s in range(shares):
+            nc.gpsimd.tensor_tensor(diff[:, s], rel[:, s, :, 0:pair], rel[:, s, :, pair:], ALU.subtract)
+        for s in range(shares):
+            nc.scalar.activation(out=excess[:, s], in_=diff[:, s], func=ACT.Relu)
+        for s in range(shares):
+            nc.gpsimd.tensor_tensor(pair_max[:, s], excess[:, s], rel[:, s, :, pair:], ALU.add)
+
+        def bank_max(h, t, skip):
             nc.vector.tensor_reduce(
-                out=top[:, t, gc],
+                out=top[:, t, h * gh + skip:(h + 1) * gh],
                 in_=banks[h, t][:, skip * EDGES:].rearrange("p (g e) -> p g e", e=EDGES),
                 axis=AX.X,
                 op=ALU.max,
             )
-            nc.scalar.activation(out=yb[:, gc, t], in_=top[:, t, gc], func=ACT.Relu, bias=bias_t[:, t:t + 1])
-            nc.scalar.activation(out=y[:, t, gc], in_=top[:, t, gc], func=ACT.Relu, bias=bias_t[:, t:t + 1])
+
+        def finish(t, g0, g1):
+            nc.scalar.activation(out=yb[:, g0:g1, t], in_=top[:, t, g0:g1], func=ACT.Relu, bias=bias_t[:, t:t + 1])
+            nc.scalar.activation(out=y[:, t, g0:g1], in_=top[:, t, g0:g1], func=ACT.Relu, bias=bias_t[:, t:t + 1])
+
+        skips = [SHARED if t in SHARED_BANKS else 0 for t in range(PACK)]
+        last_t = PACK - 1
+        for t in sorted(range(PACK), key=lambda b: skips[b]):
+            bank_max(0, t, skips[t])
+        finish(last_t, skips[last_t], gh)
+        for t in range(last_t):
+            bank_max(1, t, 0)
+            finish(t, skips[t], G)
+        nc.vector.tensor_reduce(out=y[:, 0, 0:SHARED], in_=pair_max[:, 0], axis=AX.X, op=ALU.max)
+        nc.scalar.activation(out=yb[:, 0:SHARED, 0], in_=y[:, 0, 0:SHARED], func=ACT.Copy)
+        bank_max(1, last_t, 0)
+        finish(last_t, gh, G)
         nc.vector.tensor_reduce(
-            out=yb[:, 0:SHARED, 2:],
-            in_=pair_max[:].rearrange("p u g e -> p g u e"),
-            axis=AX.X,
-            op=ALU.max,
+            out=yb[:, 0:SHARED, 2:], in_=pair_max[:, 1:].rearrange("p s g e -> p g s e"), axis=AX.X, op=ALU.max
         )
-        nc.vector.tensor_reduce(out=y[:, 2:, 0:SHARED], in_=pair_max[:], axis=AX.X, op=ALU.max)
+        nc.vector.tensor_reduce(out=y[:, 2:, 0:SHARED], in_=pair_max[:, 1:], axis=AX.X, op=ALU.max)
 
         y_codes = keep.tile([P, G], U32, name="y_codes", align_bytes=64)
         y_sc = keep.tile([P, G], U8, name="y_sc", align_bytes=64)
@@ -174,7 +196,7 @@ def tile_attend_edgeconv_pl_kernel(tc, pts_words, pts_scales, wc, wn, bias, offs
         nc.sync.dma_start(out_dealt[:, 0:2, :], y[:, 0:2, :])
         nc.scalar.dma_start(out_dealt[:, 2:, :], y[:, 2:, :])
         nc.sync.dma_start(out_1[0].rearrange("p g r -> p (g r)").bitcast(I32), y_codes[:].bitcast(I32))
-        out_rows = out_2[0].bitcast(I32).rearrange("(q r) c -> q r c", r=4)
-        for q in range(4):
+        out_rows = out_2[0].bitcast(I32).rearrange("(q r) c -> q r c", r=PACK)
+        for q in range(P // QUADRANT):
             queue = nc.sync if q % 2 == 0 else nc.scalar
-            queue.dma_start(out_rows[q], y_sc[:].bitcast(I32)[32 * q:32 * q + 4, :])
+            queue.dma_start(out_rows[q], y_sc[:].bitcast(I32)[QUADRANT * q:QUADRANT * q + PACK, :])

@@ -21,10 +21,11 @@ PACK = 4
 EDGES = I // G
 N = 512
 HALVES = I // N
+Q4 = N // 2
 LIST_ROWS = 16
 QUADRANT = 32
 WC_CHUNKS = (256, 256)
-WN_CHUNKS = (128, 192, 192)
+WN_CHUNKS = (256, 128, 128)
 SHARED = 16
 SHARED_BANKS = (0, 2, 3)
 
@@ -97,42 +98,44 @@ def tile_attend_edgeconv_pl_kernel(tc, pts_words, pts_scales, wc, wn, bias, offs
         dealt_c = round_weight(raw_c, "wc", WC_CHUNKS)
         wc_codes, wc_sc = quantise_weight(dealt_c, "wc", 1)
 
-        gw_early = keep.tile([P, N + I], U32, name="gw_early", tag=f"wc_raw{len(WC_CHUNKS) - 1}", align_bytes=64)
-        gw_c = [gw_early[:, 0:N]]
-        gw_n = [gw_early[:, (h + 1) * N:(h + 2) * N] for h in range(HALVES)]
+        gw_early = keep.tile([P, 2 * I - Q4], U32, name="gw_early", tag=f"wc_raw{len(WC_CHUNKS) - 1}", align_bytes=64)
+        gw_c = gw_early[:, 0:I - Q4]
+        gw_n = gw_early[:, I - Q4:]
         half_cols = N // LIST_ROWS
-        nc.vector.tensor_copy(gw_c[0][:], words[:].indirect(list_c[:, 0:half_cols]))
-        nc.vector.tensor_copy(gw_early[:, N:], words[:].indirect(list_n[:]))
+        nc.vector.tensor_copy(gw_c[:, 0:N], words[:].indirect(list_c[:, 0:half_cols]))
+        nc.vector.tensor_copy(gw_n, words[:].indirect(list_n[:]))
+        nc.vector.tensor_copy(gw_c[:, N:], words[:].indirect(list_c[:, half_cols:(I - Q4) // LIST_ROWS]))
 
         banks = {}
         for h in range(HALVES):
             for t in range(PACK):
                 banks[h, t] = psum.tile([P, N], F32, name=f"bank{h}{t}")
 
-        def product(h, t, codes, sc, gw, gs, opens):
+        def product(i0, n, t, codes, sc, gw, gs, opens):
             nc.tensor.matmul_mx(
-                out=banks[h, t][:],
+                out=banks[i0 // N, t][:, i0 % N:i0 % N + n],
                 lhsT=codes[:, t * P:(t + 1) * P].bitcast(FP8X4),
                 lhsT_scale=sc[:, t * P:(t + 1) * P],
-                rhs=gw[h][:].bitcast(FP8X4),
-                rhs_scale=gs[:, h * N:(h + 1) * N],
+                rhs=gw.bitcast(FP8X4),
+                rhs_scale=gs[:, i0:i0 + n],
                 start=opens,
                 stop=not opens,
             )
 
         for t in range(PACK):
-            product(0, t, wc_codes, wc_sc, gw_c, gs_c, True)
+            product(0, N, t, wc_codes, wc_sc, gw_c[:, 0:N], gs_c, True)
 
         dealt_n = round_weight(raw_n, "wn", WN_CHUNKS)
         wn_codes, wn_sc = quantise_weight(dealt_n, "wn", PACK)
-        gw_c.append(keep.tile([P, N], U32, name="gw_c1", tag=f"wn_raw{len(WN_CHUNKS) - 1}", align_bytes=64))
-        nc.vector.tensor_copy(gw_c[1][:], words[:].indirect(list_c[:, half_cols:]))
+        gw_late = keep.tile([P, Q4], U32, name="gw_late", tag=f"wn_raw{len(WN_CHUNKS) - 1}", align_bytes=64)
+        nc.vector.tensor_copy(gw_late[:], words[:].indirect(list_c[:, (I - Q4) // LIST_ROWS:]))
 
         for t in range(PACK):
-            product(0, t, wn_codes, wn_sc, gw_n, gs_n, False)
+            product(0, N, t, wn_codes, wn_sc, gw_n[:, 0:N], gs_n, False)
         for t in range(PACK):
-            product(1, t, wn_codes, wn_sc, gw_n, gs_n, True)
-            product(1, t, wc_codes, wc_sc, gw_c, gs_c, False)
+            for i0, centre in ((N, gw_c[:, N:]), (N + Q4, gw_late[:])):
+                product(i0, Q4, t, wn_codes, wn_sc, gw_n[:, i0:i0 + Q4], gs_n, True)
+                product(i0, Q4, t, wc_codes, wc_sc, centre, gs_c, False)
 
         top = keep.tile([P, PACK, G], F32, name="top")
         y = keep.tile([P, PACK, G], F32, name="y")

@@ -24,7 +24,7 @@ HALVES = I // N
 Q4 = N // 2
 LIST_ROWS = 16
 QUADRANT = 32
-WC_CHUNKS = (256, 256)
+WC_CHUNKS = (512,)
 WN_CHUNKS = (256, 128, 128)
 SHARED = 16
 SHARED_BANKS = (0, 2, 3)
@@ -96,15 +96,15 @@ def tile_attend_edgeconv_pl_kernel(tc, pts_words, pts_scales, wc, wn, bias, offs
         nc.vector.tensor_copy(gs_c[:], scales[:].indirect(list_c[:]))
 
         dealt_c = round_weight(raw_c, "wc", WC_CHUNKS)
-        wc_codes, wc_sc = quantise_weight(dealt_c, "wc", 1)
+        wc_codes, wc_sc = quantise_weight(dealt_c, "wc", 2)
 
-        gw_early = keep.tile([P, 2 * I - Q4], U32, name="gw_early", tag=f"wc_raw{len(WC_CHUNKS) - 1}", align_bytes=64)
-        gw_c = gw_early[:, 0:I - Q4]
-        gw_n = gw_early[:, I - Q4:]
+        gw_first = keep.tile([P, N], U32, name="gw_first", align_bytes=64)
+        gw_early = keep.tile([P, I + Q4], U32, name="gw_early", tag=f"wc_raw{len(WC_CHUNKS) - 1}", align_bytes=64)
+        gw_n = gw_early[:, 0:I]
         half_cols = N // LIST_ROWS
-        nc.vector.tensor_copy(gw_c[:, 0:N], words[:].indirect(list_c[:, 0:half_cols]))
+        nc.vector.tensor_copy(gw_first[:], words[:].indirect(list_c[:, 0:half_cols]))
         nc.vector.tensor_copy(gw_n, words[:].indirect(list_n[:]))
-        nc.vector.tensor_copy(gw_c[:, N:], words[:].indirect(list_c[:, half_cols:(I - Q4) // LIST_ROWS]))
+        nc.vector.tensor_copy(gw_early[:, I:], words[:].indirect(list_c[:, half_cols:(I - Q4) // LIST_ROWS]))
 
         banks = {}
         for h in range(HALVES):
@@ -123,7 +123,7 @@ def tile_attend_edgeconv_pl_kernel(tc, pts_words, pts_scales, wc, wn, bias, offs
             )
 
         for t in range(PACK):
-            product(0, N, t, wc_codes, wc_sc, gw_c[:, 0:N], gs_c, True)
+            product(0, N, t, wc_codes, wc_sc, gw_first[:], gs_c, True)
 
         dealt_n = round_weight(raw_n, "wn", WN_CHUNKS)
         wn_codes, wn_sc = quantise_weight(dealt_n, "wn", PACK)
@@ -133,7 +133,7 @@ def tile_attend_edgeconv_pl_kernel(tc, pts_words, pts_scales, wc, wn, bias, offs
         for t in range(PACK):
             product(0, N, t, wn_codes, wn_sc, gw_n[:, 0:N], gs_n, False)
         for t in range(PACK):
-            for i0, centre in ((N, gw_c[:, N:]), (N + Q4, gw_late[:])):
+            for i0, centre in ((N, gw_early[:, I:]), (N + Q4, gw_late[:])):
                 product(i0, Q4, t, wn_codes, wn_sc, gw_n[:, i0:i0 + Q4], gs_n, True)
                 product(i0, Q4, t, wc_codes, wc_sc, centre, gs_c, False)
 

@@ -21,10 +21,8 @@ PACK = 4
 EDGES = I // G
 N = 512
 HALVES = I // N
-Q4 = N // 2
 LIST_ROWS = 16
 QUADRANT = 32
-WC_CHUNKS = (512,)
 WN_CHUNKS = (256, 128, 128)
 SHARED = 16
 SHARED_BANKS = (0, 2, 3)
@@ -58,7 +56,11 @@ def tile_attend_edgeconv_pl_kernel(tc, pts_words, pts_scales, wc, wn, bias, offs
                 raws.append(raw)
             return raws
 
-        raw_c = load_weight(wc, "wc", WC_CHUNKS)
+        raw_c = []
+        for u in range(2):
+            raw = keep.tile([P, 2, F], F32, name=f"wc_raw{u}", tag=f"wc_raw{u}", align_bytes=64)
+            nc.sync.dma_start(raw[:], wc.rearrange("(p j) f -> p j f", j=PACK)[:, 2 * u:2 * u + 2, :])
+            raw_c.append(raw)
         words = keep.tile([P, T], U32, name="words", align_bytes=64)
         nc.sync.dma_start(words[:].bitcast(I32), pts_words[0].rearrange("p c r -> p (c r)").bitcast(I32))
         raw_n = load_weight(wn, "wn", WN_CHUNKS)
@@ -81,8 +83,8 @@ def tile_attend_edgeconv_pl_kernel(tc, pts_words, pts_scales, wc, wn, bias, offs
             codes = keep.tile([P, F], U32, name=f"{name}_codes", align_bytes=64)
             sc = keep.tile([P, F], U8, name=f"{name}_scales", align_bytes=64)
             flat = dealt[:].rearrange("p t m j -> p (t m j)")
-            width = F // pieces
-            for s in range(pieces):
+            width = F // len(pieces)
+            for s in pieces:
                 nc.vector.quantize_mx(
                     out=codes[:, s * width:(s + 1) * width].bitcast(FP8X4),
                     scales=sc[:, s * width:(s + 1) * width],
@@ -95,47 +97,50 @@ def tile_attend_edgeconv_pl_kernel(tc, pts_words, pts_scales, wc, wn, bias, offs
         nc.vector.tensor_copy(gs_n[:], scales[:].indirect(list_n[:]))
         nc.vector.tensor_copy(gs_c[:], scales[:].indirect(list_c[:]))
 
-        dealt_c = round_weight(raw_c, "wc", WC_CHUNKS)
-        wc_codes, wc_sc = quantise_weight(dealt_c, "wc", 2)
+        dealt_c = keep.tile([P, PACK, P, PACK], BF16, name="wc_dealt", align_bytes=64)
+        for u, t0, t1 in ((0, 0, PACK), (1, 0, 2), (1, 2, PACK)):
+            nc.scalar.copy(
+                dealt_c[:, t0:t1, :, 2 * u:2 * u + 2].rearrange("p t (a i) j -> p a t i j", i=2),
+                raw_c[u][:].rearrange("p j (a i t) -> p a t i j", i=2, t=PACK)[:, :, t0:t1],
+            )
+        wc_codes, wc_sc = quantise_weight(dealt_c, "wc", range(2))
 
-        gw_first = keep.tile([P, N], U32, name="gw_first", align_bytes=64)
-        gw_early = keep.tile([P, I + Q4], U32, name="gw_early", tag=f"wc_raw{len(WC_CHUNKS) - 1}", align_bytes=64)
-        gw_n = gw_early[:, 0:I]
+        gw_c = [keep.tile([P, N], U32, name="gw_c0", align_bytes=64)]
+        gw_all = keep.tile([P, I], U32, name="gw_all", tag="wc_raw1", align_bytes=64)
+        gw_n = [gw_all[:, h * N:(h + 1) * N] for h in range(HALVES)]
         half_cols = N // LIST_ROWS
-        nc.vector.tensor_copy(gw_first[:], words[:].indirect(list_c[:, 0:half_cols]))
-        nc.vector.tensor_copy(gw_n, words[:].indirect(list_n[:]))
-        nc.vector.tensor_copy(gw_early[:, I:], words[:].indirect(list_c[:, half_cols:(I - Q4) // LIST_ROWS]))
+        nc.vector.tensor_copy(gw_c[0][:], words[:].indirect(list_c[:, 0:half_cols]))
+        nc.vector.tensor_copy(gw_all[:], words[:].indirect(list_n[:]))
 
         banks = {}
         for h in range(HALVES):
             for t in range(PACK):
                 banks[h, t] = psum.tile([P, N], F32, name=f"bank{h}{t}")
 
-        def product(i0, n, t, codes, sc, gw, gs, opens):
+        def product(h, t, codes, sc, gw, gs, opens):
             nc.tensor.matmul_mx(
-                out=banks[i0 // N, t][:, i0 % N:i0 % N + n],
+                out=banks[h, t][:],
                 lhsT=codes[:, t * P:(t + 1) * P].bitcast(FP8X4),
                 lhsT_scale=sc[:, t * P:(t + 1) * P],
-                rhs=gw.bitcast(FP8X4),
-                rhs_scale=gs[:, i0:i0 + n],
+                rhs=gw[h][:].bitcast(FP8X4),
+                rhs_scale=gs[:, h * N:(h + 1) * N],
                 start=opens,
                 stop=not opens,
             )
 
         for t in range(PACK):
-            product(0, N, t, wc_codes, wc_sc, gw_first[:], gs_c, True)
+            product(0, t, wc_codes, wc_sc, gw_c, gs_c, True)
 
         dealt_n = round_weight(raw_n, "wn", WN_CHUNKS)
-        wn_codes, wn_sc = quantise_weight(dealt_n, "wn", PACK)
-        gw_late = keep.tile([P, Q4], U32, name="gw_late", tag=f"wn_raw{len(WN_CHUNKS) - 1}", align_bytes=64)
-        nc.vector.tensor_copy(gw_late[:], words[:].indirect(list_c[:, (I - Q4) // LIST_ROWS:]))
+        wn_codes, wn_sc = quantise_weight(dealt_n, "wn", [2 * t + u for u in range(2) for t in range(PACK)])
+        gw_c.append(keep.tile([P, N], U32, name="gw_c1", tag=f"wn_raw{len(WN_CHUNKS) - 1}", align_bytes=64))
+        nc.vector.tensor_copy(gw_c[1][:], words[:].indirect(list_c[:, half_cols:]))
 
         for t in range(PACK):
-            product(0, N, t, wn_codes, wn_sc, gw_n[:, 0:N], gs_n, False)
+            product(0, t, wn_codes, wn_sc, gw_n, gs_n, False)
         for t in range(PACK):
-            for i0, centre in ((N, gw_early[:, I:]), (N + Q4, gw_late[:])):
-                product(i0, Q4, t, wn_codes, wn_sc, gw_n[:, i0:i0 + Q4], gs_n, True)
-                product(i0, Q4, t, wc_codes, wc_sc, centre, gs_c, False)
+            product(1, t, wn_codes, wn_sc, gw_n, gs_n, True)
+            product(1, t, wc_codes, wc_sc, gw_c, gs_c, False)
 
         top = keep.tile([P, PACK, G], F32, name="top")
         y = keep.tile([P, PACK, G], F32, name="y")
@@ -159,7 +164,7 @@ def tile_attend_edgeconv_pl_kernel(tc, pts_words, pts_scales, wc, wn, bias, offs
             nc.gpsimd.tensor_tensor(diff[:, s], rel[:, s, :, 0:pair], rel[:, s, :, pair:], ALU.subtract)
         for s in range(shares):
             nc.scalar.activation(out=excess[:, s], in_=diff[:, s], func=ACT.Relu)
-        for s in range(shares):
+        for s in (slice(0, 1), slice(1, shares)):
             nc.gpsimd.tensor_tensor(pair_max[:, s], excess[:, s], rel[:, s, :, pair:], ALU.add)
 
         def bank_max(h, t, skip):

@@ -36,8 +36,15 @@ def tile_attend_edgeconv_pl_kernel(tc, pts_words, pts_scales, wc, wn, bias, offs
 
         list_c = keep.tile([P, I // LIST_ROWS], U16, name="list_c")
         list_n = keep.tile([P, I // LIST_ROWS], U16, name="list_n")
-        nc.sync.dma_start(list_c[:], offs2)
         nc.sync.dma_start(list_n[:], offs)
+
+        def load_pair(name, u, f0, f1):
+            raw = keep.tile([P, 2, f1 - f0], F32, name=name, tag=name, align_bytes=64)
+            nc.sync.dma_start(raw[:], wc.rearrange("(p j) f -> p j f", j=PACK)[:, 2 * u:2 * u + 2, f0:f1])
+            return raw
+
+        raw_a0 = load_pair("wc_a0", 0, 0, F // 2)
+        nc.sync.dma_start(list_c[:], offs2)
 
         scales = keep.tile([P, T], U8, name="scales", align_bytes=64)
         nc.vector.memset(scales[:].bitcast(I32), 0)
@@ -56,11 +63,8 @@ def tile_attend_edgeconv_pl_kernel(tc, pts_words, pts_scales, wc, wn, bias, offs
                 raws.append(raw)
             return raws
 
-        raw_c = []
-        for u in range(2):
-            raw = keep.tile([P, 2, F], F32, name=f"wc_raw{u}", tag=f"wc_raw{u}", align_bytes=64)
-            nc.sync.dma_start(raw[:], wc.rearrange("(p j) f -> p j f", j=PACK)[:, 2 * u:2 * u + 2, :])
-            raw_c.append(raw)
+        raw_a1 = load_pair("wc_a1", 0, F // 2, F)
+        raw_b = load_pair("wc_raw1", 1, 0, F)
         words = keep.tile([P, T], U32, name="words", align_bytes=64)
         nc.sync.dma_start(words[:].bitcast(I32), pts_words[0].rearrange("p c r -> p (c r)").bitcast(I32))
         raw_n = load_weight(wn, "wn", WN_CHUNKS)
@@ -98,10 +102,15 @@ def tile_attend_edgeconv_pl_kernel(tc, pts_words, pts_scales, wc, wn, bias, offs
         nc.vector.tensor_copy(gs_c[:], scales[:].indirect(list_c[:]))
 
         dealt_c = keep.tile([P, PACK, P, PACK], BF16, name="wc_dealt", align_bytes=64)
-        for u, t0, t1 in ((0, 0, PACK), (1, 0, 2), (1, 2, PACK)):
+        for raw, u, m0, m1, t0, t1 in (
+            (raw_a0, 0, 0, P // 2, 0, PACK),
+            (raw_a1, 0, P // 2, P, 0, PACK),
+            (raw_b, 1, 0, P, 0, 2),
+            (raw_b, 1, 0, P, 2, PACK),
+        ):
             nc.scalar.copy(
-                dealt_c[:, t0:t1, :, 2 * u:2 * u + 2].rearrange("p t (a i) j -> p a t i j", i=2),
-                raw_c[u][:].rearrange("p j (a i t) -> p a t i j", i=2, t=PACK)[:, :, t0:t1],
+                dealt_c[:, t0:t1, m0:m1, 2 * u:2 * u + 2].rearrange("p t (a i) j -> p a t i j", i=2),
+                raw[:].rearrange("p j (a i t) -> p a t i j", i=2, t=PACK)[:, :, t0:t1],
             )
         wc_codes, wc_sc = quantise_weight(dealt_c, "wc", range(2))
 

@@ -23,9 +23,9 @@ N = 512
 HALVES = I // N
 LIST_ROWS = 16
 QUADRANT = 32
+WC_EARLY = 256
 WN_CHUNKS = (256, 128, 128)
-SHARED = 16
-SHARED_BANKS = (0, 2, 3)
+SHARED = (24, 0, 16, 16)
 
 
 def tile_attend_edgeconv_pl_kernel(tc, pts_words, pts_scales, wc, wn, bias, offs, offs2, out_0, out_1, out_2):
@@ -43,8 +43,7 @@ def tile_attend_edgeconv_pl_kernel(tc, pts_words, pts_scales, wc, wn, bias, offs
             nc.sync.dma_start(raw[:], wc.rearrange("(p j) f -> p j f", j=PACK)[:, 2 * u:2 * u + 2, f0:f1])
             return raw
 
-        raw_a0 = load_pair("wc_a0", 0, 0, F // 2)
-        nc.sync.dma_start(list_c[:], offs2)
+        raw_a0 = load_pair("wc_a0", 0, 0, WC_EARLY)
 
         scales = keep.tile([P, T], U8, name="scales", align_bytes=64)
         nc.vector.memset(scales[:].bitcast(I32), 0)
@@ -63,8 +62,9 @@ def tile_attend_edgeconv_pl_kernel(tc, pts_words, pts_scales, wc, wn, bias, offs
                 raws.append(raw)
             return raws
 
-        raw_a1 = load_pair("wc_a1", 0, F // 2, F)
-        raw_b = load_pair("wc_raw1", 1, 0, F)
+        nc.sync.dma_start(list_c[:], offs2)
+        raw_b = load_pair("wc_b", 1, 0, F)
+        raw_a1 = load_pair("wc_raw1", 0, WC_EARLY, F)
         words = keep.tile([P, T], U32, name="words", align_bytes=64)
         nc.sync.dma_start(words[:].bitcast(I32), pts_words[0].rearrange("p c r -> p (c r)").bitcast(I32))
         raw_n = load_weight(wn, "wn", WN_CHUNKS)
@@ -103,16 +103,15 @@ def tile_attend_edgeconv_pl_kernel(tc, pts_words, pts_scales, wc, wn, bias, offs
 
         dealt_c = keep.tile([P, PACK, P, PACK], BF16, name="wc_dealt", align_bytes=64)
         for raw, u, m0, m1, t0, t1 in (
-            (raw_a0, 0, 0, P // 2, 0, PACK),
-            (raw_a1, 0, P // 2, P, 0, PACK),
-            (raw_b, 1, 0, P, 0, 2),
-            (raw_b, 1, 0, P, 2, PACK),
+            (raw_a0, 0, 0, WC_EARLY // PACK, 0, PACK),
+            (raw_b, 1, 0, P, 0, PACK),
+            (raw_a1, 0, WC_EARLY // PACK, P, 0, PACK),
         ):
             nc.scalar.copy(
                 dealt_c[:, t0:t1, m0:m1, 2 * u:2 * u + 2].rearrange("p t (a i) j -> p a t i j", i=2),
                 raw[:].rearrange("p j (a i t) -> p a t i j", i=2, t=PACK)[:, :, t0:t1],
             )
-        wc_codes, wc_sc = quantise_weight(dealt_c, "wc", range(2))
+        wc_codes, wc_sc = quantise_weight(dealt_c, "wc", range(1))
 
         gw_c = [keep.tile([P, N], U32, name="gw_c0", align_bytes=64)]
         gw_all = keep.tile([P, I], U32, name="gw_all", tag="wc_raw1", align_bytes=64)
@@ -141,7 +140,7 @@ def tile_attend_edgeconv_pl_kernel(tc, pts_words, pts_scales, wc, wn, bias, offs
             product(0, t, wc_codes, wc_sc, gw_c, gs_c, True)
 
         dealt_n = round_weight(raw_n, "wn", WN_CHUNKS)
-        wn_codes, wn_sc = quantise_weight(dealt_n, "wn", [2 * t + u for u in range(2) for t in range(PACK)])
+        wn_codes, wn_sc = quantise_weight(dealt_n, "wn", range(PACK))
         gw_c.append(keep.tile([P, N], U32, name="gw_c1", tag=f"wn_raw{len(WN_CHUNKS) - 1}", align_bytes=64))
         nc.vector.tensor_copy(gw_c[1][:], words[:].indirect(list_c[:, half_cols:]))
 
@@ -157,24 +156,26 @@ def tile_attend_edgeconv_pl_kernel(tc, pts_words, pts_scales, wc, wn, bias, offs
         gh = G // HALVES
         pair = EDGES // 2
 
-        shares = len(SHARED_BANKS)
-        rel = keep.tile([P, shares, SHARED, EDGES], F32, name="rel")
-        diff = keep.tile([P, shares, SHARED, pair], F32, name="diff")
-        excess = keep.tile([P, shares, SHARED, pair], F32, name="excess")
-        pair_max = keep.tile([P, shares, SHARED, pair], F32, name="pair_max")
-        for s, t in enumerate(SHARED_BANKS):
+        starts = [sum(SHARED[:t]) for t in range(PACK + 1)]
+        rel = keep.tile([P, starts[PACK], EDGES], F32, name="rel")
+        diff = keep.tile([P, starts[PACK], pair], F32, name="diff")
+        excess = keep.tile([P, starts[PACK], pair], F32, name="excess")
+        pair_max = keep.tile([P, starts[PACK], pair], F32, name="pair_max")
+        shares = [(t, slice(starts[t], starts[t + 1])) for t in range(PACK) if SHARED[t]]
+        first, late = slice(0, starts[1]), slice(starts[2], starts[PACK])
+        for t, s in shares:
             nc.scalar.activation(
                 out=rel[:, s].rearrange("p g e -> p (g e)"),
-                in_=banks[0, t][:, 0:SHARED * EDGES],
+                in_=banks[0, t][:, 0:SHARED[t] * EDGES],
                 func=ACT.Relu,
                 bias=bias_t[:, t:t + 1],
             )
-        for s in range(shares):
-            nc.gpsimd.tensor_tensor(diff[:, s], rel[:, s, :, 0:pair], rel[:, s, :, pair:], ALU.subtract)
-        for s in range(shares):
+        for t, s in shares:
+            nc.gpsimd.tensor_tensor(diff[:, s], rel[:, s, 0:pair], rel[:, s, pair:], ALU.subtract)
+        for t, s in shares:
             nc.scalar.activation(out=excess[:, s], in_=diff[:, s], func=ACT.Relu)
-        for s in (slice(0, 1), slice(1, shares)):
-            nc.gpsimd.tensor_tensor(pair_max[:, s], excess[:, s], rel[:, s, :, pair:], ALU.add)
+        for s in (first, late):
+            nc.gpsimd.tensor_tensor(pair_max[:, s], excess[:, s], rel[:, s, pair:], ALU.add)
 
         def bank_max(h, t, skip):
             nc.vector.tensor_reduce(
@@ -188,22 +189,22 @@ def tile_attend_edgeconv_pl_kernel(tc, pts_words, pts_scales, wc, wn, bias, offs
             nc.scalar.activation(out=yb[:, g0:g1, t], in_=top[:, t, g0:g1], func=ACT.Relu, bias=bias_t[:, t:t + 1])
             nc.scalar.activation(out=y[:, t, g0:g1], in_=top[:, t, g0:g1], func=ACT.Relu, bias=bias_t[:, t:t + 1])
 
-        skips = [SHARED if t in SHARED_BANKS else 0 for t in range(PACK)]
         last_t = PACK - 1
-        for t in sorted(range(PACK), key=lambda b: skips[b]):
-            bank_max(0, t, skips[t])
-        finish(last_t, skips[last_t], gh)
+        for t in sorted(range(PACK), key=lambda b: SHARED[b]):
+            bank_max(0, t, SHARED[t])
+        finish(last_t, SHARED[last_t], gh)
         for t in range(last_t):
             bank_max(1, t, 0)
-            finish(t, skips[t], G)
-        nc.vector.tensor_reduce(out=y[:, 0, 0:SHARED], in_=pair_max[:, 0], axis=AX.X, op=ALU.max)
-        nc.scalar.activation(out=yb[:, 0:SHARED, 0], in_=y[:, 0, 0:SHARED], func=ACT.Copy)
+            finish(t, SHARED[t], G)
+        nc.vector.tensor_reduce(out=y[:, 0, 0:SHARED[0]], in_=pair_max[:, first], axis=AX.X, op=ALU.max)
+        nc.scalar.activation(out=yb[:, 0:SHARED[0], 0], in_=y[:, 0, 0:SHARED[0]], func=ACT.Copy)
         bank_max(1, last_t, 0)
         finish(last_t, gh, G)
+        late_max = pair_max[:, late].rearrange("p (s g) e -> p s g e", s=2)
         nc.vector.tensor_reduce(
-            out=yb[:, 0:SHARED, 2:], in_=pair_max[:, 1:].rearrange("p s g e -> p g s e"), axis=AX.X, op=ALU.max
+            out=yb[:, 0:SHARED[2], 2:], in_=late_max.rearrange("p s g e -> p g s e"), axis=AX.X, op=ALU.max
         )
-        nc.vector.tensor_reduce(out=y[:, 2:, 0:SHARED], in_=pair_max[:, 1:], axis=AX.X, op=ALU.max)
+        nc.vector.tensor_reduce(out=y[:, 2:, 0:SHARED[2]], in_=late_max, axis=AX.X, op=ALU.max)
 
         y_codes = keep.tile([P, G], U32, name="y_codes", align_bytes=64)
         y_sc = keep.tile([P, G], U8, name="y_sc", align_bytes=64)

@@ -25,7 +25,7 @@ LIST_ROWS = 16
 QUADRANT = 32
 WC_EARLY = 256
 WN_CHUNKS = (256, 128, 128)
-SHARED = (24, 0, 16, 16)
+SHARED = (16, 0, 16, 16)
 
 
 def tile_attend_edgeconv_pl_kernel(tc, pts_words, pts_scales, wc, wn, bias, offs, offs2, out_0, out_1, out_2):
@@ -157,7 +157,7 @@ def tile_attend_edgeconv_pl_kernel(tc, pts_words, pts_scales, wc, wn, bias, offs
         pair = EDGES // 2
 
         starts = [sum(SHARED[:t]) for t in range(PACK + 1)]
-        rel = keep.tile([P, starts[PACK], EDGES], F32, name="rel")
+        rel = keep.tile([P, 2, starts[PACK], pair], F32, name="rel")
         diff = keep.tile([P, starts[PACK], pair], F32, name="diff")
         excess = keep.tile([P, starts[PACK], pair], F32, name="excess")
         pair_max = keep.tile([P, starts[PACK], pair], F32, name="pair_max")
@@ -165,17 +165,17 @@ def tile_attend_edgeconv_pl_kernel(tc, pts_words, pts_scales, wc, wn, bias, offs
         first, late = slice(0, starts[1]), slice(starts[2], starts[PACK])
         for t, s in shares:
             nc.scalar.activation(
-                out=rel[:, s].rearrange("p g e -> p (g e)"),
-                in_=banks[0, t][:, 0:SHARED[t] * EDGES],
+                out=rel[:, :, s].rearrange("p u g e -> p g u e"),
+                in_=banks[0, t][:, 0:SHARED[t] * EDGES].rearrange("p (g u e) -> p g u e", u=2, e=pair),
                 func=ACT.Relu,
                 bias=bias_t[:, t:t + 1],
             )
         for t, s in shares:
-            nc.gpsimd.tensor_tensor(diff[:, s], rel[:, s, 0:pair], rel[:, s, pair:], ALU.subtract)
+            nc.gpsimd.tensor_tensor(diff[:, s], rel[:, 0, s], rel[:, 1, s], ALU.subtract)
         for t, s in shares:
             nc.scalar.activation(out=excess[:, s], in_=diff[:, s], func=ACT.Relu)
         for s in (first, late):
-            nc.gpsimd.tensor_tensor(pair_max[:, s], excess[:, s], rel[:, s, pair:], ALU.add)
+            nc.gpsimd.tensor_tensor(pair_max[:, s], excess[:, s], rel[:, 1, s], ALU.add)
 
         def bank_max(h, t, skip):
             nc.vector.tensor_reduce(

@@ -25,7 +25,7 @@ LIST_ROWS = 16
 QUADRANT = 32
 WC_EARLY = 256
 WN_CHUNKS = (256, 128, 128)
-SHARED = (16, 0, 16, 16)
+SHARED = (16, 0, 12, 12)
 
 
 def tile_attend_edgeconv_pl_kernel(tc, pts_words, pts_scales, wc, wn, bias, offs, offs2, out_0, out_1, out_2):

@@ -24,7 +24,7 @@ HALVES = I // N
 LIST_ROWS = 16
 QUADRANT = 32
 WC_EARLY = 256
-WN_CHUNKS = (256, 128, 128)
+WN_CHUNKS = (192, 192, 128)
 SHARED = (16, 0, 12, 12)
 
 
@@ -38,12 +38,10 @@ def tile_attend_edgeconv_pl_kernel(tc, pts_words, pts_scales, wc, wn, bias, offs
         list_n = keep.tile([P, I // LIST_ROWS], U16, name="list_n")
         nc.sync.dma_start(list_n[:], offs)
 
-        def load_pair(name, u, f0, f1):
-            raw = keep.tile([P, 2, f1 - f0], F32, name=name, tag=name, align_bytes=64)
-            nc.sync.dma_start(raw[:], wc.rearrange("(p j) f -> p j f", j=PACK)[:, 2 * u:2 * u + 2, f0:f1])
-            return raw
-
-        raw_a0 = load_pair("wc_a0", 0, 0, WC_EARLY)
+        raw_c = keep.tile([P, PACK, F], F32, name="wc_raw", tag="wc_raw", align_bytes=64)
+        wc_rows = wc.rearrange("(p j) f -> p j f", j=PACK)
+        raw_early = keep.tile([P, 2, WC_EARLY], F32, name="wc_early", align_bytes=64)
+        nc.sync.dma_start(raw_early[:], wc_rows[:, 0:2, 0:WC_EARLY])
 
         scales = keep.tile([P, T], U8, name="scales", align_bytes=64)
         nc.vector.memset(scales[:].bitcast(I32), 0)
@@ -63,8 +61,8 @@ def tile_attend_edgeconv_pl_kernel(tc, pts_words, pts_scales, wc, wn, bias, offs
             return raws
 
         nc.sync.dma_start(list_c[:], offs2)
-        raw_b = load_pair("wc_b", 1, 0, F)
-        raw_a1 = load_pair("wc_raw1", 0, WC_EARLY, F)
+        nc.sync.dma_start(raw_c[:, 2:, :], wc_rows[:, 2:, :])
+        nc.sync.dma_start(raw_c[:, 0:2, WC_EARLY:], wc_rows[:, 0:2, WC_EARLY:])
         words = keep.tile([P, T], U32, name="words", align_bytes=64)
         nc.sync.dma_start(words[:].bitcast(I32), pts_words[0].rearrange("p c r -> p (c r)").bitcast(I32))
         raw_n = load_weight(wn, "wn", WN_CHUNKS)
@@ -102,19 +100,22 @@ def tile_attend_edgeconv_pl_kernel(tc, pts_words, pts_scales, wc, wn, bias, offs
         nc.vector.tensor_copy(gs_c[:], scales[:].indirect(list_c[:]))
 
         dealt_c = keep.tile([P, PACK, P, PACK], BF16, name="wc_dealt", align_bytes=64)
-        for raw, u, m0, m1, t0, t1 in (
-            (raw_a0, 0, 0, WC_EARLY // PACK, 0, PACK),
-            (raw_b, 1, 0, P, 0, PACK),
-            (raw_a1, 0, WC_EARLY // PACK, P, 0, PACK),
-        ):
+        m_early = WC_EARLY // PACK
+        for j0, pair_of_rows in ((0, raw_early[:]), (2, raw_c[:, 2:, 0:WC_EARLY])):
             nc.scalar.copy(
-                dealt_c[:, t0:t1, m0:m1, 2 * u:2 * u + 2].rearrange("p t (a i) j -> p a t i j", i=2),
-                raw[:].rearrange("p j (a i t) -> p a t i j", i=2, t=PACK)[:, :, t0:t1],
+                dealt_c[:, :, 0:m_early, j0:j0 + 2].rearrange("p t (a i) j -> p a t i j", i=2),
+                pair_of_rows.rearrange("p j (a i t) -> p a t i j", i=2, t=PACK),
+            )
+        for t0 in range(0, PACK, 2):
+            nc.scalar.activation(
+                out=dealt_c[:, t0:t0 + 2, m_early:, :].rearrange("p t m j -> p m j t"),
+                in_=raw_c[:, :, WC_EARLY:].rearrange("p j (m t) -> p m j t", t=PACK)[:, :, :, t0:t0 + 2],
+                func=ACT.Copy,
             )
         wc_codes, wc_sc = quantise_weight(dealt_c, "wc", range(1))
 
         gw_c = [keep.tile([P, N], U32, name="gw_c0", align_bytes=64)]
-        gw_all = keep.tile([P, I], U32, name="gw_all", tag="wc_raw1", align_bytes=64)
+        gw_all = keep.tile([P, I], U32, name="gw_all", tag="wc_raw", align_bytes=64)
         gw_n = [gw_all[:, h * N:(h + 1) * N] for h in range(HALVES)]
         half_cols = N // LIST_ROWS
         nc.vector.tensor_copy(gw_c[0][:], words[:].indirect(list_c[:, 0:half_cols]))

@@ -25,6 +25,7 @@ LIST_ROWS = 16
 QUADRANT = 32
 WC_EARLY = 256
 WN_CHUNKS = (192, 192, 128)
+LENT = (192, 64, 0)
 SHARED = (16, 0, 12, 12)
 
 
@@ -73,11 +74,20 @@ def tile_attend_edgeconv_pl_kernel(tc, pts_words, pts_scales, wc, wn, bias, offs
             dealt = keep.tile([P, PACK, P, PACK], BF16, name=f"{name}_dealt", align_bytes=64)
             for c, width in enumerate(widths):
                 m0 = sum(widths[:c]) // PACK
-                for t0 in range(0, PACK, 2):
-                    nc.scalar.activation(
-                        out=dealt[:, t0:t0 + 2, m0:m0 + width // PACK, :].rearrange("p t m j -> p m j t"),
-                        in_=raws[c][:].rearrange("p j (m t) -> p m j t", t=PACK)[:, :, :, t0:t0 + 2],
-                        func=ACT.Copy,
+                mw = width // PACK
+                src = raws[c][:].rearrange("p j (m t) -> p m j t", t=PACK)
+                lent = LENT[c] // PACK
+                for t0, lo in ((0, 0), (2, lent)):
+                    if lo < mw:
+                        nc.scalar.activation(
+                            out=dealt[:, t0:t0 + 2, m0 + lo:m0 + mw, :].rearrange("p t m j -> p m j t"),
+                            in_=src[:, lo:, :, t0:t0 + 2],
+                            func=ACT.Copy,
+                        )
+                if lent:
+                    nc.gpsimd.tensor_scalar(
+                        dealt[:, 2:, m0:m0 + lent, :],
+                        src[:, 0:lent, :, 2:].rearrange("p m j t -> p t m j"), 1.0, 0.0, ALU.mult, ALU.add,
                     )
             return dealt
 

@@ -26,6 +26,7 @@ QUADRANT = 32
 WC_EARLY = 256
 WN_CHUNKS = (192, 192, 128)
 LENT = (192, 64, 0)
+WC_LENT = 192
 SHARED = (16, 0, 12, 12)
 
 
@@ -116,12 +117,18 @@ def tile_attend_edgeconv_pl_kernel(tc, pts_words, pts_scales, wc, wn, bias, offs
                 dealt_c[:, :, 0:m_early, j0:j0 + 2].rearrange("p t (a i) j -> p a t i j", i=2),
                 pair_of_rows.rearrange("p j (a i t) -> p a t i j", i=2, t=PACK),
             )
-        for t0 in range(0, PACK, 2):
+        late_c = raw_c[:, :, WC_EARLY:].rearrange("p j (m t) -> p m j t", t=PACK)
+        lent_c = WC_LENT // PACK
+        for t0, lo in ((0, 0), (2, lent_c)):
             nc.scalar.activation(
-                out=dealt_c[:, t0:t0 + 2, m_early:, :].rearrange("p t m j -> p m j t"),
-                in_=raw_c[:, :, WC_EARLY:].rearrange("p j (m t) -> p m j t", t=PACK)[:, :, :, t0:t0 + 2],
+                out=dealt_c[:, t0:t0 + 2, m_early + lo:, :].rearrange("p t m j -> p m j t"),
+                in_=late_c[:, lo:, :, t0:t0 + 2],
                 func=ACT.Copy,
             )
+        nc.gpsimd.tensor_scalar(
+            dealt_c[:, 2:, m_early:m_early + lent_c, :],
+            late_c[:, 0:lent_c, :, 2:].rearrange("p m j t -> p t m j"), 1.0, 0.0, ALU.mult, ALU.add,
+        )
         wc_codes, wc_sc = quantise_weight(dealt_c, "wc", range(1))
 
         gw_c = [keep.tile([P, N], U32, name="gw_c0", align_bytes=64)]

@@ -24,8 +24,9 @@ HALVES = I // N
 LIST_ROWS = 16
 QUADRANT = 32
 WC_EARLY = 256
-WN_CHUNKS = (192, 192, 128)
-LENT = (192, 64, 0)
+HALF_F = F // 2
+WN_SPLIT = 384
+WN_LENT = 192
 WC_LENT = 192
 SHARED = (16, 0, 12, 12)
 
@@ -52,45 +53,40 @@ def tile_attend_edgeconv_pl_kernel(tc, pts_words, pts_scales, wc, wn, bias, offs
             queue = nc.sync if r % 2 == 0 else nc.scalar
             queue.dma_start(scales[:].bitcast(I32)[r:P:QUADRANT, :], scale_rows[r])
 
-        def load_weight(w, name, widths):
-            rows = w.rearrange("(p j) f -> p j f", j=PACK)
-            raws = []
-            for c, width in enumerate(widths):
-                f0 = sum(widths[:c])
-                raw = keep.tile([P, PACK, width], F32, name=f"{name}_raw{c}", tag=f"{name}_raw{c}", align_bytes=64)
-                nc.sync.dma_start(raw[:], rows[:, :, f0:f0 + width])
-                raws.append(raw)
-            return raws
-
         nc.sync.dma_start(list_c[:], offs2)
         nc.sync.dma_start(raw_c[:, 2:, :], wc_rows[:, 2:, :])
         nc.sync.dma_start(raw_c[:, 0:2, WC_EARLY:], wc_rows[:, 0:2, WC_EARLY:])
         words = keep.tile([P, T], U32, name="words", align_bytes=64)
         nc.sync.dma_start(words[:].bitcast(I32), pts_words[0].rearrange("p c r -> p (c r)").bitcast(I32))
-        raw_n = load_weight(wn, "wn", WN_CHUNKS)
+        wn_rows = wn.rearrange("(p j) f -> p j f", j=PACK)
+        raw_n = keep.tile([P, PACK, F], F32, name="wn_raw", align_bytes=64)
+        raw_last = keep.tile([P, 2, HALF_F], F32, name="wn_last", tag="wn_last", align_bytes=64)
+        nc.sync.dma_start(raw_n[:, 0:2, :], wn_rows[:, 0:2, :])
+        nc.sync.dma_start(raw_n[:, 2:, 0:HALF_F], wn_rows[:, 2:, 0:HALF_F])
+        nc.sync.dma_start(raw_last[:], wn_rows[:, 2:, HALF_F:])
         bias_t = keep.tile([P, PACK], F32, name="bias_t")
         nc.sync.dma_start(bias_t[:], bias.rearrange("(p t) o -> p (t o)", t=PACK))
 
-        def round_weight(raws, name, widths):
-            dealt = keep.tile([P, PACK, P, PACK], BF16, name=f"{name}_dealt", align_bytes=64)
-            for c, width in enumerate(widths):
-                m0 = sum(widths[:c]) // PACK
-                mw = width // PACK
-                src = raws[c][:].rearrange("p j (m t) -> p m j t", t=PACK)
-                lent = LENT[c] // PACK
-                for t0, lo in ((0, 0), (2, lent)):
-                    if lo < mw:
-                        nc.scalar.activation(
-                            out=dealt[:, t0:t0 + 2, m0 + lo:m0 + mw, :].rearrange("p t m j -> p m j t"),
-                            in_=src[:, lo:, :, t0:t0 + 2],
-                            func=ACT.Copy,
-                        )
-                if lent:
-                    nc.gpsimd.tensor_scalar(
-                        dealt[:, 2:, m0:m0 + lent, :],
-                        src[:, 0:lent, :, 2:].rearrange("p m j t -> p t m j"), 1.0, 0.0, ALU.mult, ALU.add,
-                    )
-            return dealt
+        def round_lines(dealt, raw, f0, f1, t0):
+            nc.scalar.activation(
+                out=dealt[:, t0:t0 + 2, f0 // PACK:f1 // PACK, :].rearrange("p t m j -> p m j t"),
+                in_=raw[:, :, f0:f1].rearrange("p j (m t) -> p m j t", t=PACK)[:, :, :, t0:t0 + 2],
+                func=ACT.Copy,
+            )
+
+        def round_pair(dealt, rows, f0, j0, t0, t1):
+            m0, mw = f0 // PACK, rows.shape[2] // PACK
+            nc.scalar.copy(
+                dealt[:, t0:t1, m0:m0 + mw, j0:j0 + 2].rearrange("p t (a i) j -> p a t i j", i=2),
+                rows.rearrange("p j (a i t) -> p a t i j", i=2, t=PACK)[:, :, t0:t1],
+            )
+
+        def round_lent(dealt, rows, f0, j0, t0):
+            m0, mw = f0 // PACK, rows.shape[2] // PACK
+            nc.gpsimd.tensor_scalar(
+                dealt[:, t0:, m0:m0 + mw, j0:j0 + rows.shape[1]],
+                rows.rearrange("p j (m t) -> p t m j", t=PACK)[:, t0:], 1.0, 0.0, ALU.mult, ALU.add,
+            )
 
         def quantise_weight(dealt, name, pieces):
             codes = keep.tile([P, F], U32, name=f"{name}_codes", align_bytes=64)
@@ -157,9 +153,16 @@ def tile_attend_edgeconv_pl_kernel(tc, pts_words, pts_scales, wc, wn, bias, offs
         for t in range(PACK):
             product(0, t, wc_codes, wc_sc, gw_c, gs_c, True)
 
-        dealt_n = round_weight(raw_n, "wn", WN_CHUNKS)
+        dealt_n = keep.tile([P, PACK, P, PACK], BF16, name="wn_dealt", align_bytes=64)
+        round_pair(dealt_n, raw_n[:, 0:2, HALF_F:WN_SPLIT], HALF_F, 0, 0, PACK)
+        round_lent(dealt_n, raw_n[:, 0:2, WN_SPLIT:], WN_SPLIT, 0, 0)
+        round_lines(dealt_n, raw_n, 0, HALF_F, 0)
+        round_lent(dealt_n, raw_n[:, :, 0:WN_LENT], 0, 0, 2)
+        round_lines(dealt_n, raw_n, WN_LENT, HALF_F, 2)
+        for t0 in range(0, PACK, 2):
+            round_pair(dealt_n, raw_last[:], HALF_F, 2, t0, t0 + 2)
         wn_codes, wn_sc = quantise_weight(dealt_n, "wn", range(PACK))
-        gw_c.append(keep.tile([P, N], U32, name="gw_c1", tag=f"wn_raw{len(WN_CHUNKS) - 1}", align_bytes=64))
+        gw_c.append(keep.tile([P, N], U32, name="gw_c1", tag="wn_last", align_bytes=64))
         nc.vector.tensor_copy(gw_c[1][:], words[:].indirect(list_c[:, half_cols:]))
 
         for t in range(PACK):

@@ -23,28 +23,28 @@ N = 512
 HALVES = I // N
 LIST_ROWS = 16
 QUADRANT = 32
-WC_EARLY = 256
+WC_EARLY = 64
 HALF_F = F // 2
 WN_SPLIT = 384
 WN_LENT = 192
-WC_LENT = 192
-SHARED = (16, 0, 12, 12)
+WC_SPLIT = 320
+SHARED = (32, 0, 12, 12)
 
 
 def tile_attend_edgeconv_pl_kernel(tc, pts_words, pts_scales, wc, wn, bias, offs, offs2, out_0, out_1, out_2):
     nc = tc.nc
     with ExitStack() as ctx:
         keep = ctx.enter_context(tc.tile_pool(name="keep", bufs=1))
+        reuse = ctx.enter_context(tc.tile_pool(name="reuse", bufs=1))
         psum = ctx.enter_context(tc.psum_pool(name="psum", bufs=1))
 
         list_c = keep.tile([P, I // LIST_ROWS], U16, name="list_c")
         list_n = keep.tile([P, I // LIST_ROWS], U16, name="list_n")
         nc.sync.dma_start(list_n[:], offs)
 
-        raw_c = keep.tile([P, PACK, F], F32, name="wc_raw", tag="wc_raw", align_bytes=64)
+        raw_c = reuse.tile([P, PACK, F], F32, name="wc_raw", offset=0, align_bytes=64)
         wc_rows = wc.rearrange("(p j) f -> p j f", j=PACK)
-        raw_early = keep.tile([P, 2, WC_EARLY], F32, name="wc_early", align_bytes=64)
-        nc.sync.dma_start(raw_early[:], wc_rows[:, 0:2, 0:WC_EARLY])
+        nc.sync.dma_start(raw_c[:, 0, :], wc_rows[:, 0, :])
 
         scales = keep.tile([P, T], U8, name="scales", align_bytes=64)
         nc.vector.memset(scales[:].bitcast(I32), 0)
@@ -54,8 +54,8 @@ def tile_attend_edgeconv_pl_kernel(tc, pts_words, pts_scales, wc, wn, bias, offs
             queue.dma_start(scales[:].bitcast(I32)[r:P:QUADRANT, :], scale_rows[r])
 
         nc.sync.dma_start(list_c[:], offs2)
+        nc.sync.dma_start(raw_c[:, 1, :], wc_rows[:, 1, :])
         nc.sync.dma_start(raw_c[:, 2:, :], wc_rows[:, 2:, :])
-        nc.sync.dma_start(raw_c[:, 0:2, WC_EARLY:], wc_rows[:, 0:2, WC_EARLY:])
         words = keep.tile([P, T], U32, name="words", align_bytes=64)
         nc.sync.dma_start(words[:].bitcast(I32), pts_words[0].rearrange("p c r -> p (c r)").bitcast(I32))
         wn_rows = wn.rearrange("(p j) f -> p j f", j=PACK)
@@ -107,28 +107,19 @@ def tile_attend_edgeconv_pl_kernel(tc, pts_words, pts_scales, wc, wn, bias, offs
         nc.vector.tensor_copy(gs_c[:], scales[:].indirect(list_c[:]))
 
         dealt_c = keep.tile([P, PACK, P, PACK], BF16, name="wc_dealt", align_bytes=64)
-        m_early = WC_EARLY // PACK
-        for j0, pair_of_rows in ((0, raw_early[:]), (2, raw_c[:, 2:, 0:WC_EARLY])):
+        for j in range(2):
             nc.scalar.copy(
-                dealt_c[:, :, 0:m_early, j0:j0 + 2].rearrange("p t (a i) j -> p a t i j", i=2),
-                pair_of_rows.rearrange("p j (a i t) -> p a t i j", i=2, t=PACK),
+                dealt_c[:, :, 0:WC_EARLY // PACK, j],
+                raw_c[:, j, 0:WC_EARLY].rearrange("p (m t) -> p t m", t=PACK),
             )
-        late_c = raw_c[:, :, WC_EARLY:].rearrange("p j (m t) -> p m j t", t=PACK)
-        lent_c = WC_LENT // PACK
-        for t0, lo in ((0, 0), (2, lent_c)):
-            nc.scalar.activation(
-                out=dealt_c[:, t0:t0 + 2, m_early + lo:, :].rearrange("p t m j -> p m j t"),
-                in_=late_c[:, lo:, :, t0:t0 + 2],
-                func=ACT.Copy,
-            )
-        nc.gpsimd.tensor_scalar(
-            dealt_c[:, 2:, m_early:m_early + lent_c, :],
-            late_c[:, 0:lent_c, :, 2:].rearrange("p m j t -> p t m j"), 1.0, 0.0, ALU.mult, ALU.add,
-        )
+        round_pair(dealt_c, raw_c[:, 0:2, WC_EARLY:WC_SPLIT], WC_EARLY, 0, 0, PACK)
+        round_lent(dealt_c, raw_c[:, 0:2, WC_SPLIT:], WC_SPLIT, 0, 0)
+        round_pair(dealt_c, raw_c[:, 2:, 0:WC_SPLIT], 0, 2, 0, PACK)
+        round_lent(dealt_c, raw_c[:, 2:, WC_SPLIT:], WC_SPLIT, 2, 0)
         wc_codes, wc_sc = quantise_weight(dealt_c, "wc", range(1))
 
-        gw_c = [keep.tile([P, N], U32, name="gw_c0", align_bytes=64)]
-        gw_all = keep.tile([P, I], U32, name="gw_all", tag="wc_raw", align_bytes=64)
+        gw_c = [reuse.tile([P, N], U32, name="gw_c0", offset=4 * I, align_bytes=64)]
+        gw_all = reuse.tile([P, I], U32, name="gw_all", offset=0, align_bytes=64)
         gw_n = [gw_all[:, h * N:(h + 1) * N] for h in range(HALVES)]
         half_cols = N // LIST_ROWS
         nc.vector.tensor_copy(gw_c[0][:], words[:].indirect(list_c[:, 0:half_cols]))
@@ -191,9 +182,9 @@ def tile_attend_edgeconv_pl_kernel(tc, pts_words, pts_scales, wc, wn, bias, offs
                 func=ACT.Relu,
                 bias=bias_t[:, t:t + 1],
             )
-        for t, s in shares:
+        for s in (first, late):
             nc.gpsimd.tensor_tensor(diff[:, s], rel[:, 0, s], rel[:, 1, s], ALU.subtract)
-        for t, s in shares:
+        for s in (first, late):
             nc.scalar.activation(out=excess[:, s], in_=diff[:, s], func=ACT.Relu)
         for s in (first, late):
             nc.gpsimd.tensor_tensor(pair_max[:, s], excess[:, s], rel[:, 1, s], ALU.add)
@@ -211,7 +202,7 @@ def tile_attend_edgeconv_pl_kernel(tc, pts_words, pts_scales, wc, wn, bias, offs
             nc.scalar.activation(out=y[:, t, g0:g1], in_=top[:, t, g0:g1], func=ACT.Relu, bias=bias_t[:, t:t + 1])
 
         last_t = PACK - 1
-        for t in sorted(range(PACK), key=lambda b: SHARED[b]):
+        for t in range(1, PACK):
             bank_max(0, t, SHARED[t])
         finish(last_t, SHARED[last_t], gh)
         for t in range(last_t):

@@ -28,7 +28,7 @@ HALF_F = F // 2
 WN_SPLIT = 384
 WN_LENT = 192
 WC_SPLIT = 320
-SHARED = (32, 0, 12, 12)
+SHARED = (16, 0, 12, 12)
 
 
 def tile_attend_edgeconv_pl_kernel(tc, pts_words, pts_scales, wc, wn, bias, offs, offs2, out_0, out_1, out_2):
@@ -182,9 +182,9 @@ def tile_attend_edgeconv_pl_kernel(tc, pts_words, pts_scales, wc, wn, bias, offs
                 func=ACT.Relu,
                 bias=bias_t[:, t:t + 1],
             )
-        for s in (first, late):
+        for t, s in shares:
             nc.gpsimd.tensor_tensor(diff[:, s], rel[:, 0, s], rel[:, 1, s], ALU.subtract)
-        for s in (first, late):
+        for t, s in shares:
             nc.scalar.activation(out=excess[:, s], in_=diff[:, s], func=ACT.Relu)
         for s in (first, late):
             nc.gpsimd.tensor_tensor(pair_max[:, s], excess[:, s], rel[:, 1, s], ALU.add)
@@ -202,7 +202,7 @@ def tile_attend_edgeconv_pl_kernel(tc, pts_words, pts_scales, wc, wn, bias, offs
             nc.scalar.activation(out=y[:, t, g0:g1], in_=top[:, t, g0:g1], func=ACT.Relu, bias=bias_t[:, t:t + 1])
 
         last_t = PACK - 1
-        for t in range(1, PACK):
+        for t in sorted(range(PACK), key=lambda b: SHARED[b]):
             bank_max(0, t, SHARED[t])
         finish(last_t, SHARED[last_t], gh)
         for t in range(last_t):

@@ -141,6 +141,16 @@ def tile_attend_edgeconv_pl_kernel(tc, pts_words, pts_scales, wc, wn, bias, offs
                 stop=not opens,
             )
 
+        nc.tensor.matmul_mx(
+            out=banks[HALVES - 1, PACK - 1][:],
+            lhsT=wc_codes[:, 0:P].bitcast(FP8X4),
+            lhsT_scale=wc_sc[:, 0:P],
+            rhs=wc_codes[:].bitcast(FP8X4),
+            rhs_scale=wc_sc[:],
+            start=True,
+            stop=True,
+        )
+
         for t in range(PACK):
             product(0, t, wc_codes, wc_sc, gw_c, gs_c, True)
 

@@ -25,8 +25,6 @@ LIST_ROWS = 16
 QUADRANT = 32
 WC_EARLY = 64
 HALF_F = F // 2
-WN_SPLIT = 384
-WN_LENT = 192
 WC_SPLIT = 320
 SHARED = (16, 0, 12, 12)
 
@@ -38,15 +36,15 @@ def tile_attend_edgeconv_pl_kernel(tc, pts_words, pts_scales, wc, wn, bias, offs
         reuse = ctx.enter_context(tc.tile_pool(name="reuse", bufs=1))
         psum = ctx.enter_context(tc.psum_pool(name="psum", bufs=1))
 
-        list_c = keep.tile([P, I // LIST_ROWS], U16, name="list_c")
-        list_n = keep.tile([P, I // LIST_ROWS], U16, name="list_n")
+        list_c = keep.tile([P, I // LIST_ROWS], U16, name="list_c", align_bytes=256)
+        list_n = keep.tile([P, I // LIST_ROWS], U16, name="list_n", align_bytes=256)
         nc.sync.dma_start(list_n[:], offs)
 
-        raw_c = reuse.tile([P, PACK, F], F32, name="wc_raw", offset=0, align_bytes=64)
+        raw_c = reuse.tile([P, PACK, F], F32, name="wc_raw", offset=0, align_bytes=256)
         wc_rows = wc.rearrange("(p j) f -> p j f", j=PACK)
         nc.sync.dma_start(raw_c[:, 0, :], wc_rows[:, 0, :])
 
-        scales = keep.tile([P, T], U8, name="scales", align_bytes=64)
+        scales = keep.tile([P, T], U8, name="scales", align_bytes=256)
         nc.vector.memset(scales[:].bitcast(I32), 0)
         scale_rows = pts_scales[0].bitcast(I32).rearrange("(q r) c -> r q c", r=PACK)
         for r in range(PACK):
@@ -56,23 +54,15 @@ def tile_attend_edgeconv_pl_kernel(tc, pts_words, pts_scales, wc, wn, bias, offs
         nc.sync.dma_start(list_c[:], offs2)
         nc.sync.dma_start(raw_c[:, 1, :], wc_rows[:, 1, :])
         nc.sync.dma_start(raw_c[:, 2:, :], wc_rows[:, 2:, :])
-        words = keep.tile([P, T], U32, name="words", align_bytes=64)
+        words = keep.tile([P, T], U32, name="words", align_bytes=256)
         nc.sync.dma_start(words[:].bitcast(I32), pts_words[0].rearrange("p c r -> p (c r)").bitcast(I32))
-        wn_rows = wn.rearrange("(p j) f -> p j f", j=PACK)
-        raw_n = keep.tile([P, PACK, F], F32, name="wn_raw", align_bytes=64)
-        raw_last = keep.tile([P, 2, HALF_F], F32, name="wn_last", tag="wn_last", align_bytes=64)
-        nc.sync.dma_start(raw_n[:, 0:2, :], wn_rows[:, 0:2, :])
-        nc.sync.dma_start(raw_n[:, 2:, 0:HALF_F], wn_rows[:, 2:, 0:HALF_F])
-        nc.sync.dma_start(raw_last[:], wn_rows[:, 2:, HALF_F:])
+        wn_flat = wn.rearrange("(p j) f -> p (j f)", j=PACK)
+        raw_n = keep.tile([P, PACK, F], F32, name="wn_raw", tag="wn_raw", align_bytes=256)
+        flat_n = raw_n[:].rearrange("p j f -> p (j f)")
+        for c0, c1 in ((0, 2 * F), (2 * F, PACK * F - HALF_F), (PACK * F - HALF_F, PACK * F)):
+            nc.sync.dma_start(flat_n[:, c0:c1], wn_flat[:, c0:c1])
         bias_t = keep.tile([P, PACK], F32, name="bias_t")
         nc.sync.dma_start(bias_t[:], bias.rearrange("(p t) o -> p (t o)", t=PACK))
-
-        def round_lines(dealt, raw, f0, f1, t0):
-            nc.scalar.activation(
-                out=dealt[:, t0:t0 + 2, f0 // PACK:f1 // PACK, :].rearrange("p t m j -> p m j t"),
-                in_=raw[:, :, f0:f1].rearrange("p j (m t) -> p m j t", t=PACK)[:, :, :, t0:t0 + 2],
-                func=ACT.Copy,
-            )
 
         def round_pair(dealt, rows, f0, j0, t0, t1):
             m0, mw = f0 // PACK, rows.shape[2] // PACK
@@ -155,15 +145,14 @@ def tile_attend_edgeconv_pl_kernel(tc, pts_words, pts_scales, wc, wn, bias, offs
             product(0, t, wc_codes, wc_sc, gw_c, gs_c, True)
 
         dealt_n = keep.tile([P, PACK, P, PACK], BF16, name="wn_dealt", align_bytes=64)
-        round_pair(dealt_n, raw_n[:, 0:2, HALF_F:WN_SPLIT], HALF_F, 0, 0, PACK)
-        round_lent(dealt_n, raw_n[:, 0:2, WN_SPLIT:], WN_SPLIT, 0, 0)
-        round_lines(dealt_n, raw_n, 0, HALF_F, 0)
-        round_lent(dealt_n, raw_n[:, :, 0:WN_LENT], 0, 0, 2)
-        round_lines(dealt_n, raw_n, WN_LENT, HALF_F, 2)
+        round_pair(dealt_n, raw_n[:, 0:2, 0:WC_SPLIT], 0, 0, 0, PACK)
+        round_lent(dealt_n, raw_n[:, 0:2, WC_SPLIT:], WC_SPLIT, 0, 0)
+        round_pair(dealt_n, raw_n[:, 2:, 0:HALF_F], 0, 2, 0, 2)
+        round_lent(dealt_n, raw_n[:, 2:, 0:HALF_F], 0, 2, 2)
         for t0 in range(0, PACK, 2):
-            round_pair(dealt_n, raw_last[:], HALF_F, 2, t0, t0 + 2)
+            round_pair(dealt_n, raw_n[:, 2:, HALF_F:], HALF_F, 2, t0, t0 + 2)
         wn_codes, wn_sc = quantise_weight(dealt_n, "wn", range(PACK))
-        gw_c.append(keep.tile([P, N], U32, name="gw_c1", tag="wn_last", align_bytes=64))
+        gw_c.append(keep.tile([P, N], U32, name="gw_c1", tag="wn_raw", align_bytes=256))
         nc.vector.tensor_copy(gw_c[1][:], words[:].indirect(list_c[:, half_cols:]))
 
         for t in range(PACK):

@@ -223,7 +223,7 @@ def tile_attend_edgeconv_pl_kernel(tc, pts_words, pts_scales, wc, wn, bias, offs
 
         out_dealt = out_0.rearrange("(p t) g -> p t g", t=PACK)
         nc.sync.dma_start(out_dealt[:, 0:2, :], y[:, 0:2, :])
-        nc.scalar.dma_start(out_dealt[:, 2:, :], y[:, 2:, :])
+        nc.sync.dma_start(out_dealt[:, 2:, :], y[:, 2:, :])
         nc.sync.dma_start(out_1[0].rearrange("p g r -> p (g r)").bitcast(I32), y_codes[:].bitcast(I32))
         out_rows = out_2[0].bitcast(I32).rearrange("(q r) c -> q r c", r=PACK)
         for q in range(P // QUADRANT):

@@ -23,7 +23,8 @@ N = 512
 HALVES = I // N
 LIST_ROWS = 16
 QUADRANT = 32
-WC_EARLY = 64
+PRELOAD = 256
+N_EARLY = 256
 HALF_F = F // 2
 WC_SPLIT = 320
 SHARED = (16, 0, 12, 12)
@@ -40,9 +41,11 @@ def tile_attend_edgeconv_pl_kernel(tc, pts_words, pts_scales, wc, wn, bias, offs
         list_n = keep.tile([P, I // LIST_ROWS], U16, name="list_n", align_bytes=256)
         nc.sync.dma_start(list_n[:], offs)
 
-        raw_c = reuse.tile([P, PACK, F], F32, name="wc_raw", offset=0, align_bytes=256)
+        raw_c = keep.tile([P, 2, F], F32, name="wc_raw", align_bytes=256)
         wc_rows = wc.rearrange("(p j) f -> p j f", j=PACK)
-        nc.sync.dma_start(raw_c[:, 0, :], wc_rows[:, 0, :])
+        wc_flat = wc.rearrange("(p j) f -> p (j f)", j=PACK)
+        flat_c = raw_c[:].rearrange("p j f -> p (j f)")
+        nc.sync.dma_start(flat_c[:, 0:PRELOAD], wc_flat[:, 0:PRELOAD])
 
         scales = keep.tile([P, T], U8, name="scales", align_bytes=256)
         nc.vector.memset(scales[:].bitcast(I32), 0)
@@ -52,10 +55,13 @@ def tile_attend_edgeconv_pl_kernel(tc, pts_words, pts_scales, wc, wn, bias, offs
             queue.dma_start(scales[:].bitcast(I32)[r:P:QUADRANT, :], scale_rows[r])
 
         nc.sync.dma_start(list_c[:], offs2)
-        nc.sync.dma_start(raw_c[:, 1, :], wc_rows[:, 1, :])
-        nc.sync.dma_start(raw_c[:, 2:, :], wc_rows[:, 2:, :])
+        nc.sync.dma_start(flat_c[:, PRELOAD:], wc_flat[:, PRELOAD:2 * F])
         words = keep.tile([P, T], U32, name="words", align_bytes=256)
         nc.sync.dma_start(words[:].bitcast(I32), pts_words[0].rearrange("p c r -> p (c r)").bitcast(I32))
+        left_c = keep.tile([P, 2, HALF_F], F32, name="wc_left", align_bytes=256)
+        right_c = reuse.tile([P, 2, HALF_F], F32, name="wc_right", offset=0, align_bytes=256)
+        nc.sync.dma_start(left_c[:], wc_rows[:, 2:, 0:HALF_F])
+        nc.sync.dma_start(right_c[:], wc_rows[:, 2:, HALF_F:])
         wn_flat = wn.rearrange("(p j) f -> p (j f)", j=PACK)
         raw_n = keep.tile([P, PACK, F], F32, name="wn_raw", tag="wn_raw", align_bytes=256)
         flat_n = raw_n[:].rearrange("p j f -> p (j f)")
@@ -97,52 +103,40 @@ def tile_attend_edgeconv_pl_kernel(tc, pts_words, pts_scales, wc, wn, bias, offs
         nc.vector.tensor_copy(gs_c[:], scales[:].indirect(list_c[:]))
 
         dealt_c = keep.tile([P, PACK, P, PACK], BF16, name="wc_dealt", align_bytes=64)
-        for j in range(2):
-            nc.scalar.copy(
-                dealt_c[:, :, 0:WC_EARLY // PACK, j],
-                raw_c[:, j, 0:WC_EARLY].rearrange("p (m t) -> p t m", t=PACK),
-            )
-        round_pair(dealt_c, raw_c[:, 0:2, WC_EARLY:WC_SPLIT], WC_EARLY, 0, 0, PACK)
-        round_lent(dealt_c, raw_c[:, 0:2, WC_SPLIT:], WC_SPLIT, 0, 0)
-        round_pair(dealt_c, raw_c[:, 2:, 0:WC_SPLIT], 0, 2, 0, PACK)
-        round_lent(dealt_c, raw_c[:, 2:, WC_SPLIT:], WC_SPLIT, 2, 0)
-        wc_codes, wc_sc = quantise_weight(dealt_c, "wc", range(1))
+        round_pair(dealt_c, raw_c[:, :, 0:WC_SPLIT], 0, 0, 0, PACK)
+        round_lent(dealt_c, raw_c[:, :, WC_SPLIT:], WC_SPLIT, 0, 0)
+        round_pair(dealt_c, left_c[:], 0, 2, 0, PACK)
+        round_pair(dealt_c, right_c[:], HALF_F, 2, 0, 2)
+        round_lent(dealt_c, right_c[:], HALF_F, 2, 2)
 
-        gw_c = [reuse.tile([P, N], U32, name="gw_c0", offset=4 * I, align_bytes=64)]
-        gw_all = reuse.tile([P, I], U32, name="gw_all", offset=0, align_bytes=64)
-        gw_n = [gw_all[:, h * N:(h + 1) * N] for h in range(HALVES)]
         half_cols = N // LIST_ROWS
+        early_cols = N_EARLY // LIST_ROWS
+        gw_c = [keep.tile([P, N], U32, name="gw_c0", align_bytes=64)]
+        gw_early = keep.tile([P, N_EARLY], U32, name="gw_early", align_bytes=64)
         nc.vector.tensor_copy(gw_c[0][:], words[:].indirect(list_c[:, 0:half_cols]))
-        nc.vector.tensor_copy(gw_all[:], words[:].indirect(list_n[:]))
+        nc.vector.tensor_copy(gw_early[:], words[:].indirect(list_n[:, 0:early_cols]))
+        wc_codes, wc_sc = quantise_weight(dealt_c, "wc", range(2))
+        gw_rest = reuse.tile([P, I - N_EARLY], U32, name="gw_rest", offset=0, align_bytes=64)
+        nc.vector.tensor_copy(gw_rest[:], words[:].indirect(list_n[:, early_cols:]))
 
         banks = {}
         for h in range(HALVES):
             for t in range(PACK):
                 banks[h, t] = psum.tile([P, N], F32, name=f"bank{h}{t}")
 
-        def product(h, t, codes, sc, gw, gs, opens):
+        def product(h, t, e0, e1, codes, sc, gw, gs, start, stop):
             nc.tensor.matmul_mx(
-                out=banks[h, t][:],
+                out=banks[h, t][:, e0:e1],
                 lhsT=codes[:, t * P:(t + 1) * P].bitcast(FP8X4),
                 lhsT_scale=sc[:, t * P:(t + 1) * P],
-                rhs=gw[h][:].bitcast(FP8X4),
-                rhs_scale=gs[:, h * N:(h + 1) * N],
-                start=opens,
-                stop=not opens,
+                rhs=gw.bitcast(FP8X4),
+                rhs_scale=gs[:, h * N + e0:h * N + e1],
+                start=start,
+                stop=stop,
             )
 
-        nc.tensor.matmul_mx(
-            out=banks[HALVES - 1, PACK - 1][:],
-            lhsT=wc_codes[:, 0:P].bitcast(FP8X4),
-            lhsT_scale=wc_sc[:, 0:P],
-            rhs=wc_codes[:].bitcast(FP8X4),
-            rhs_scale=wc_sc[:],
-            start=True,
-            stop=True,
-        )
-
         for t in range(PACK):
-            product(0, t, wc_codes, wc_sc, gw_c, gs_c, True)
+            product(0, t, 0, N, wc_codes, wc_sc, gw_c[0][:], gs_c, True, False)
 
         dealt_n = keep.tile([P, PACK, P, PACK], BF16, name="wn_dealt", align_bytes=64)
         round_pair(dealt_n, raw_n[:, 0:2, 0:WC_SPLIT], 0, 0, 0, PACK)
@@ -156,10 +150,11 @@ def tile_attend_edgeconv_pl_kernel(tc, pts_words, pts_scales, wc, wn, bias, offs
         nc.vector.tensor_copy(gw_c[1][:], words[:].indirect(list_c[:, half_cols:]))
 
         for t in range(PACK):
-            product(0, t, wn_codes, wn_sc, gw_n, gs_n, False)
+            product(0, t, 0, N_EARLY, wn_codes, wn_sc, gw_early[:], gs_n, False, False)
+            product(0, t, N_EARLY, N, wn_codes, wn_sc, gw_rest[:, 0:N - N_EARLY], gs_n, False, True)
         for t in range(PACK):
-            product(1, t, wn_codes, wn_sc, gw_n, gs_n, True)
-            product(1, t, wc_codes, wc_sc, gw_c, gs_c, False)
+            product(1, t, 0, N, wn_codes, wn_sc, gw_rest[:, N - N_EARLY:], gs_n, True, False)
+            product(1, t, 0, N, wc_codes, wc_sc, gw_c[1][:], gs_c, False, True)
 
         top = keep.tile([P, PACK, G], F32, name="top")
         y = keep.tile([P, PACK, G], F32, name="y")

@@ -23,7 +23,7 @@ N = 512
 HALVES = I // N
 LIST_ROWS = 16
 QUADRANT = 32
-PRELOAD = 256
+PRELOAD = 512
 N_EARLY = 256
 HALF_F = F // 2
 WC_SPLIT = 320

from contextlib import ExitStack

import concourse.mybir as mybir

K, T, I, F, G = 512, 2048, 1024, 512, 64
FLOPS = 2 * 2 * K * F * I

F32 = mybir.dt.float32
BF16 = mybir.dt.bfloat16
I32 = mybir.dt.int32
U32 = mybir.dt.uint32
U16 = mybir.dt.uint16
U8 = mybir.dt.uint8
FP8X4 = mybir.dt.float8_e4m3fn_x4
ACT = mybir.ActivationFunctionType
ALU = mybir.AluOpType
AX = mybir.AxisListType

P = 128
PACK = 4
EDGES = I // G
N = 512
HALVES = I // N
LIST_ROWS = 16
QUADRANT = 32
PRELOAD = 512
N_EARLY = 256
HALF_F = F // 2
WC_SPLIT = 320
SHARED = (16, 0, 12, 12)


def tile_attend_edgeconv_pl_kernel(tc, pts_words, pts_scales, wc, wn, bias, offs, offs2, out_0, out_1, out_2):
    nc = tc.nc
    with ExitStack() as ctx:
        keep = ctx.enter_context(tc.tile_pool(name="keep", bufs=1))
        reuse = ctx.enter_context(tc.tile_pool(name="reuse", bufs=1))
        psum = ctx.enter_context(tc.psum_pool(name="psum", bufs=1))

        list_c = keep.tile([P, I // LIST_ROWS], U16, name="list_c", align_bytes=256)
        list_n = keep.tile([P, I // LIST_ROWS], U16, name="list_n", align_bytes=256)
        nc.sync.dma_start(list_n[:], offs)

        raw_c = keep.tile([P, 2, F], F32, name="wc_raw", align_bytes=256)
        wc_rows = wc.rearrange("(p j) f -> p j f", j=PACK)
        wc_flat = wc.rearrange("(p j) f -> p (j f)", j=PACK)
        flat_c = raw_c[:].rearrange("p j f -> p (j f)")
        nc.sync.dma_start(flat_c[:, 0:PRELOAD], wc_flat[:, 0:PRELOAD])

        scales = keep.tile([P, T], U8, name="scales", align_bytes=256)
        nc.vector.memset(scales[:].bitcast(I32), 0)
        scale_rows = pts_scales[0].bitcast(I32).rearrange("(q r) c -> r q c", r=PACK)
        for r in range(PACK):
            queue = nc.sync if r % 2 == 0 else nc.scalar
            queue.dma_start(scales[:].bitcast(I32)[r:P:QUADRANT, :], scale_rows[r])

        nc.sync.dma_start(list_c[:], offs2)
        nc.sync.dma_start(flat_c[:, PRELOAD:], wc_flat[:, PRELOAD:2 * F])
        words = keep.tile([P, T], U32, name="words", align_bytes=256)
        nc.sync.dma_start(words[:].bitcast(I32), pts_words[0].rearrange("p c r -> p (c r)").bitcast(I32))
        left_c = keep.tile([P, 2, HALF_F], F32, name="wc_left", align_bytes=256)
        right_c = reuse.tile([P, 2, HALF_F], F32, name="wc_right", offset=0, align_bytes=256)
        nc.sync.dma_start(left_c[:], wc_rows[:, 2:, 0:HALF_F])
        nc.sync.dma_start(right_c[:], wc_rows[:, 2:, HALF_F:])
        wn_flat = wn.rearrange("(p j) f -> p (j f)", j=PACK)
        raw_n = keep.tile([P, PACK, F], F32, name="wn_raw", tag="wn_raw", align_bytes=256)
        flat_n = raw_n[:].rearrange("p j f -> p (j f)")
        for c0, c1 in ((0, 2 * F), (2 * F, PACK * F - HALF_F), (PACK * F - HALF_F, PACK * F)):
            nc.sync.dma_start(flat_n[:, c0:c1], wn_flat[:, c0:c1])
        bias_t = keep.tile([P, PACK], F32, name="bias_t")
        nc.sync.dma_start(bias_t[:], bias.rearrange("(p t) o -> p (t o)", t=PACK))

        def round_pair(dealt, rows, f0, j0, t0, t1):
            m0, mw = f0 // PACK, rows.shape[2] // PACK
            nc.scalar.copy(
                dealt[:, t0:t1, m0:m0 + mw, j0:j0 + 2].rearrange("p t (a i) j -> p a t i j", i=2),
                rows.rearrange("p j (a i t) -> p a t i j", i=2, t=PACK)[:, :, t0:t1],
            )

        def round_lent(dealt, rows, f0, j0, t0):
            m0, mw = f0 // PACK, rows.shape[2] // PACK
            nc.gpsimd.tensor_scalar(
                dealt[:, t0:, m0:m0 + mw, j0:j0 + rows.shape[1]],
                rows.rearrange("p j (m t) -> p t m j", t=PACK)[:, t0:], 1.0, 0.0, ALU.mult, ALU.add,
            )

        def quantise_weight(dealt, name, pieces):
            codes = keep.tile([P, F], U32, name=f"{name}_codes", align_bytes=64)
            sc = keep.tile([P, F], U8, name=f"{name}_scales", align_bytes=64)
            flat = dealt[:].rearrange("p t m j -> p (t m j)")
            width = F // len(pieces)
            for s in pieces:
                nc.vector.quantize_mx(
                    out=codes[:, s * width:(s + 1) * width].bitcast(FP8X4),
                    scales=sc[:, s * width:(s + 1) * width],
                    in_=flat[:, s * width * PACK:(s + 1) * width * PACK],
                )
            return codes, sc

        gs_c = keep.tile([P, I], U8, name="gs_c", align_bytes=64)
        gs_n = keep.tile([P, I], U8, name="gs_n", align_bytes=64)
        nc.vector.tensor_copy(gs_n[:], scales[:].indirect(list_n[:]))
        nc.vector.tensor_copy(gs_c[:], scales[:].indirect(list_c[:]))

        dealt_c = keep.tile([P, PACK, P, PACK], BF16, name="wc_dealt", align_bytes=64)
        round_pair(dealt_c, raw_c[:, :, 0:WC_SPLIT], 0, 0, 0, PACK)
        round_lent(dealt_c, raw_c[:, :, WC_SPLIT:], WC_SPLIT, 0, 0)
        round_pair(dealt_c, left_c[:], 0, 2, 0, PACK)
        round_pair(dealt_c, right_c[:], HALF_F, 2, 0, 2)
        round_lent(dealt_c, right_c[:], HALF_F, 2, 2)

        half_cols = N // LIST_ROWS
        early_cols = N_EARLY // LIST_ROWS
        gw_c = [keep.tile([P, N], U32, name="gw_c0", align_bytes=64)]
        gw_early = keep.tile([P, N_EARLY], U32, name="gw_early", align_bytes=64)
        nc.vector.tensor_copy(gw_c[0][:], words[:].indirect(list_c[:, 0:half_cols]))
        nc.vector.tensor_copy(gw_early[:], words[:].indirect(list_n[:, 0:early_cols]))
        wc_codes, wc_sc = quantise_weight(dealt_c, "wc", range(2))
        gw_rest = reuse.tile([P, I - N_EARLY], U32, name="gw_rest", offset=0, align_bytes=64)
        nc.vector.tensor_copy(gw_rest[:], words[:].indirect(list_n[:, early_cols:]))

        banks = {}
        for h in range(HALVES):
            for t in range(PACK):
                banks[h, t] = psum.tile([P, N], F32, name=f"bank{h}{t}")

        def product(h, t, e0, e1, codes, sc, gw, gs, start, stop):
            nc.tensor.matmul_mx(
                out=banks[h, t][:, e0:e1],
                lhsT=codes[:, t * P:(t + 1) * P].bitcast(FP8X4),
                lhsT_scale=sc[:, t * P:(t + 1) * P],
                rhs=gw.bitcast(FP8X4),
                rhs_scale=gs[:, h * N + e0:h * N + e1],
                start=start,
                stop=stop,
            )

        for t in range(PACK):
            product(0, t, 0, N, wc_codes, wc_sc, gw_c[0][:], gs_c, True, False)

        dealt_n = keep.tile([P, PACK, P, PACK], BF16, name="wn_dealt", align_bytes=64)
        round_pair(dealt_n, raw_n[:, 0:2, 0:WC_SPLIT], 0, 0, 0, PACK)
        round_lent(dealt_n, raw_n[:, 0:2, WC_SPLIT:], WC_SPLIT, 0, 0)
        round_pair(dealt_n, raw_n[:, 2:, 0:HALF_F], 0, 2, 0, 2)
        round_lent(dealt_n, raw_n[:, 2:, 0:HALF_F], 0, 2, 2)
        for t0 in range(0, PACK, 2):
            round_pair(dealt_n, raw_n[:, 2:, HALF_F:], HALF_F, 2, t0, t0 + 2)
        wn_codes, wn_sc = quantise_weight(dealt_n, "wn", range(PACK))
        gw_c.append(keep.tile([P, N], U32, name="gw_c1", tag="wn_raw", align_bytes=256))
        nc.vector.tensor_copy(gw_c[1][:], words[:].indirect(list_c[:, half_cols:]))

        for t in range(PACK):
            product(0, t, 0, N_EARLY, wn_codes, wn_sc, gw_early[:], gs_n, False, False)
            product(0, t, N_EARLY, N, wn_codes, wn_sc, gw_rest[:, 0:N - N_EARLY], gs_n, False, True)
        for t in range(PACK):
            product(1, t, 0, N, wn_codes, wn_sc, gw_rest[:, N - N_EARLY:], gs_n, True, False)
            product(1, t, 0, N, wc_codes, wc_sc, gw_c[1][:], gs_c, False, True)

        top = keep.tile([P, PACK, G], F32, name="top")
        y = keep.tile([P, PACK, G], F32, name="y")
        yb = keep.tile([P, G, PACK], BF16, name="yb", align_bytes=64)
        gh = G // HALVES
        pair = EDGES // 2

        starts = [sum(SHARED[:t]) for t in range(PACK + 1)]
        rel = keep.tile([P, 2, starts[PACK], pair], F32, name="rel")
        diff = keep.tile([P, starts[PACK], pair], F32, name="diff")
        excess = keep.tile([P, starts[PACK], pair], F32, name="excess")
        pair_max = keep.tile([P, starts[PACK], pair], F32, name="pair_max")
        shares = [(t, slice(starts[t], starts[t + 1])) for t in range(PACK) if SHARED[t]]
        first, late = slice(0, starts[1]), slice(starts[2], starts[PACK])
        for t, s in shares:
            nc.scalar.activation(
                out=rel[:, :, s].rearrange("p u g e -> p g u e"),
                in_=banks[0, t][:, 0:SHARED[t] * EDGES].rearrange("p (g u e) -> p g u e", u=2, e=pair),
                func=ACT.Relu,
                bias=bias_t[:, t:t + 1],
            )
        for t, s in shares:
            nc.gpsimd.tensor_tensor(diff[:, s], rel[:, 0, s], rel[:, 1, s], ALU.subtract)
        for t, s in shares:
            nc.scalar.activation(out=excess[:, s], in_=diff[:, s], func=ACT.Relu)
        for s in (first, late):
            nc.gpsimd.tensor_tensor(pair_max[:, s], excess[:, s], rel[:, 1, s], ALU.add)

        def bank_max(h, t, skip):
            nc.vector.tensor_reduce(
                out=top[:, t, h * gh + skip:(h + 1) * gh],
                in_=banks[h, t][:, skip * EDGES:].rearrange("p (g e) -> p g e", e=EDGES),
                axis=AX.X,
                op=ALU.max,
            )

        def finish(t, g0, g1):
            nc.scalar.activation(out=yb[:, g0:g1, t], in_=top[:, t, g0:g1], func=ACT.Relu, bias=bias_t[:, t:t + 1])
            nc.scalar.activation(out=y[:, t, g0:g1], in_=top[:, t, g0:g1], func=ACT.Relu, bias=bias_t[:, t:t + 1])

        last_t = PACK - 1
        for t in sorted(range(PACK), key=lambda b: SHARED[b]):
            bank_max(0, t, SHARED[t])
        finish(last_t, SHARED[last_t], gh)
        for t in range(last_t):
            bank_max(1, t, 0)
            finish(t, SHARED[t], G)
        nc.vector.tensor_reduce(out=y[:, 0, 0:SHARED[0]], in_=pair_max[:, first], axis=AX.X, op=ALU.max)
        nc.scalar.activation(out=yb[:, 0:SHARED[0], 0], in_=y[:, 0, 0:SHARED[0]], func=ACT.Copy)
        bank_max(1, last_t, 0)
        finish(last_t, gh, G)
        late_max = pair_max[:, late].rearrange("p (s g) e -> p s g e", s=2)
        nc.vector.tensor_reduce(
            out=yb[:, 0:SHARED[2], 2:], in_=late_max.rearrange("p s g e -> p g s e"), axis=AX.X, op=ALU.max
        )
        nc.vector.tensor_reduce(out=y[:, 2:, 0:SHARED[2]], in_=late_max, axis=AX.X, op=ALU.max)

        y_codes = keep.tile([P, G], U32, name="y_codes", align_bytes=64)
        y_sc = keep.tile([P, G], U8, name="y_sc", align_bytes=64)
        nc.vector.quantize_mx(out=y_codes[:].bitcast(FP8X4), scales=y_sc[:], in_=yb[:].rearrange("p g t -> p (g t)"))

        out_dealt = out_0.rearrange("(p t) g -> p t g", t=PACK)
        nc.sync.dma_start(out_dealt[:, 0:2, :], y[:, 0:2, :])
        nc.sync.dma_start(out_dealt[:, 2:, :], y[:, 2:, :])
        nc.sync.dma_start(out_1[0].rearrange("p g r -> p (g r)").bitcast(I32), y_codes[:].bitcast(I32))
        out_rows = out_2[0].bitcast(I32).rearrange("(q r) c -> q r c", r=PACK)
        for q in range(P // QUADRANT):
            queue = nc.sync if q % 2 == 0 else nc.scalar
            queue.dma_start(out_rows[q], y_sc[:].bitcast(I32)[QUADRANT * q:QUADRANT * q + PACK, :])
